import numpy as np
import ml_dtypes


def mxq(x, axis, fmt="e4m3"):
    dtype, down = {"e4m3": (ml_dtypes.float8_e4m3fn, 7), "e5m2": (ml_dtypes.float8_e5m2, 14)}[fmt]
    v = np.moveaxis(np.asarray(x, np.float32).astype(ml_dtypes.bfloat16).astype(np.float64), axis, -1)
    blocks = v.reshape(v.shape[:-1] + (-1, 32))
    amax = np.abs(blocks).max(-1, keepdims=True)
    byte = np.maximum(np.where(amax > 0, np.frexp(amax)[1] - 1 + 127, 0) - down, 1)
    scale = np.exp2(byte - 127.0)
    codes = (blocks / scale).astype(np.float32).astype(dtype).astype(np.float64)
    return np.moveaxis((codes * scale).reshape(v.shape), -1, axis)


WIDE = False


def mx_kscale(k):
    if not WIDE:
        return np.ones(k)
    levels = np.array([10, -10, 5, -5, 0])
    if k % 512:
        return np.exp2(np.random.permutation(np.resize(levels, k // 32))).repeat(32)
    a = np.empty((k // 512, 16))
    for p in range(k // 512):
        a[p, :8] = np.random.permutation(np.resize(levels, 8))
        for g in range(8):
            far = levels[np.abs(levels - a[p, g]) >= 10]
            a[p, g + 8] = far[np.random.randint(len(far))]
    return np.exp2(a.ravel()).repeat(32)


def f64(x):
    return np.asarray(x).astype(np.float64)


def striped(idx):
    return np.tile(np.asarray(idx).reshape(-1, 16).T, (8, 1)).astype(np.uint16)


def unstriped(offs):
    return offs[:16].T.reshape(-1).astype(np.int64)


E2M1 = np.array([0.0, 0.5, 1.0, 1.5, 2.0, 3.0, 4.0, 6.0, -0.0, -0.5, -1.0, -1.5, -2.0, -3.0, -4.0, -6.0])


def pack_weight(w, fmt):
    k, n = w.shape
    w = f64(np.asarray(w, np.float32).astype(ml_dtypes.bfloat16)).reshape(k // 32, 32, n)
    amax = np.abs(w).max(1)
    if fmt == "e4m3":
        byte = np.frexp(amax)[1] - 1 + 127 - 7
    else:
        mant, ex = np.frexp(amax / 6.0)
        byte = np.where(mant > 0.5, ex, ex - 1) + 127
    byte = np.clip(np.where(amax > 0, byte, 1), 1, 254)
    scaled = (w * np.exp2(127.0 - byte)[:, None, :]).reshape(k, n).astype(np.float32)
    by_word = np.ascontiguousarray(scaled.reshape(k // 512, 128, 4, n).transpose(0, 1, 3, 2))
    if fmt == "e4m3":
        words = by_word.astype(ml_dtypes.float8_e4m3fn).view(np.uint8)
    else:
        c = by_word.astype(ml_dtypes.float4_e2m1fn).view(np.uint8) & 0xF
        words = (c[..., 0::2] | (c[..., 1::2] << 4)).reshape(k // 512, 128, 2 * n)
    return np.ascontiguousarray(words), np.ascontiguousarray(byte.astype(np.uint8).reshape(k // 512, 16, n))


def unpack_weight(words, scales, fmt):
    g, _, n = scales.shape
    words = np.ascontiguousarray(words).reshape(g, 128, n, -1)
    if fmt == "e4m3":
        vals = words.view(ml_dtypes.float8_e4m3fn).astype(np.float64)
    else:
        nib = np.empty((g, 128, n, 4), np.uint8)
        nib[..., 0::2] = words & 0xF
        nib[..., 1::2] = words >> 4
        vals = E2M1[nib]
    vals = vals * np.repeat(np.exp2(scales.astype(np.float64) - 127.0), 8, axis=1)[..., None]
    return vals.transpose(0, 1, 3, 2).reshape(g * 512, n)


def silu(v):
    return v / (1.0 + np.exp(-v))


B, N, T, D, NQ = 1, 512, 2048, 512, 512
DV = 512


def sgn(shape):
    return np.random.uniform(0.5, 2.0, shape) * np.where(np.random.standard_normal(shape) < 0, -1.0, 1.0)


def setup_inputs():
    n = np.random.standard_normal
    idx = np.random.permutation(T)[:B * N]
    s = mx_kscale(D)[:, None]
    u = mx_kscale(N)
    ut = np.ones(T)
    ut[idx] = u
    kp = pack_weight(n((D, T)) / s, "e4m3")
    cp = pack_weight(n((D, T)) / s, "e4m3")
    return {
        "qT": (n((B, D, NQ)) * s * (1.00 / np.sqrt(D))).astype(np.float32),
        "k_words": kp[0],
        "k_scales": kp[1],
        "c_words": cp[0],
        "c_scales": cp[1],
        "vT": (n((DV, T)) / ut).astype(np.float32),
        "nb": np.tile(0.5 * n(2048), (128, 1)).astype(np.float32),
        "us": (sgn((B, N, 1)) * u[:, None]).astype(np.float32),
        "offs": striped(idx),
    }


def reference(qT, k_words, k_scales, c_words, c_scales, vT, nb, us, offs):
    idx = unstriped(offs)
    pick = lambda x, which: x[:, which].reshape(x.shape[0], B, -1).transpose(1, 0, 2)
    k = unpack_weight(k_words, k_scales, "e4m3")
    kg = pick(k, idx)
    c = unpack_weight(c_words, c_scales, "e4m3")
    cg = pick(c, idx)
    qq = mxq(f64(qT), 1, "e4m3")
    a = kg.transpose(0, 2, 1) @ qq
    z = cg.transpose(0, 2, 1) @ qq
    y = silu(a + pick(f64(nb), idx)[:, :1, :].transpose(0, 2, 1)) * z * f64(us)
    wq = mxq(y, 1, "e4m3")
    o = wq.transpose(0, 2, 1) @ mxq(pick(f64(vT), idx).transpose(0, 2, 1), 1, "e4m3")
    return o

@@ -1,0 +1,201 @@
+from contextlib import ExitStack
+
+import concourse.mybir as mybir
+from concourse.masks import make_identity
+
+F32 = mybir.dt.float32
+BF16 = mybir.dt.bfloat16
+I32 = mybir.dt.int32
+U32 = mybir.dt.uint32
+U16 = mybir.dt.uint16
+U8 = mybir.dt.uint8
+FP8X4 = mybir.dt.float8_e4m3fn_x4
+ACT = mybir.ActivationFunctionType
+ALU = mybir.AluOpType
+
+P = 128
+PACK = 4
+T = 2048
+N = 512
+NQ = 512
+D = 512
+DV = 512
+HALF = NQ // 2
+FLOPS = 2 * N * NQ * (2 * D + DV)
+BYTES = 4 * D * NQ + 2 * (D * T + D * T // 32) + 4 * DV * T + 4 * T + 4 * N + 2 * N + 4 * NQ * DV
+
+
+def tile_attend_mlpb_swiglu_topk_kernel(tc, qT, k_words, k_scales, c_words, c_scales, vT, nb, us, offs, out):
+    nc = tc.nc
+    with ExitStack() as ctx:
+        keep = ctx.enter_context(tc.tile_pool(name="keep", bufs=1))
+        psum = ctx.enter_context(tc.psum_pool(name="psum", bufs=2))
+
+        def sbuf(name, shape, dtype, slot=None):
+            return keep.tile(shape, dtype, name=name, tag=slot or name, align_bytes=64)
+
+        def load_scales(queue, tile, scales):
+            for quad in range(4):
+                queue.dma_start(
+                    tile[32 * quad : 32 * quad + 4, :].bitcast(I32),
+                    scales[0, 4 * quad : 4 * quad + 4, :].bitcast(I32),
+                )
+
+        def load_words(name, words, slot):
+            tile = sbuf(name, [P, T], I32, slot)
+            nc.sync.dma_start(tile[:], words[0].rearrange("p t r -> p (t r)").bitcast(I32))
+            return tile
+
+        def load_values(j, slot):
+            tile = sbuf("v_all%d" % j, [P, T], F32, slot)
+            nc.sync.dma_start(tile[:], vT[j * P : (j + 1) * P, :])
+            return tile
+
+        def quantize(codes, plane, values, cols):
+            nc.vector.quantize_mx(
+                out=codes[:, cols].bitcast(FP8X4),
+                scales=plane[:, cols],
+                in_=values[:, cols, :].rearrange("p c t -> p (c t)"),
+            )
+
+        def matmul(acc, lhs_codes, lhs_plane, rhs_codes, rhs_plane):
+            nc.tensor.matmul_mx(
+                out=acc, lhsT=lhs_codes.bitcast(FP8X4), lhsT_scale=lhs_plane,
+                rhs=rhs_codes.bitcast(FP8X4), rhs_scale=rhs_plane, start=True, stop=True,
+            )
+
+        halves = [slice(h * HALF, (h + 1) * HALF) for h in range(2)]
+
+        offsets = keep.tile([P, N // 16], U16, name="offsets")
+        nc.sync.dma_start(offsets[:], offs)
+
+        k_sc_all = sbuf("k_sc_all", [P, T], U8, "slot_b")
+        c_sc_all = sbuf("c_sc_all", [P, T], U8, "slot_c")
+        nb_all = sbuf("nb_all", [P, T], F32, "slot_a")
+        nc.gpsimd.memset(k_sc_all[:].bitcast(I32), 0)
+        nc.gpsimd.memset(c_sc_all[:].bitcast(I32), 0)
+        nc.vector.memset(nb_all[0 : P - 1, :], 0.0)
+        warm = keep.tile([P, 2], F32, name="warm")
+        nc.vector.memset(warm[:, 0:1], 0.0)
+        q_raw = sbuf("q_raw", [P, PACK, NQ], F32)
+        us_col = keep.tile([P, PACK], F32, name="us_col")
+        ident = keep.tile([P, P], F32, name="ident")
+
+        nc.sync.dma_start(nb_all[P - 1 : P, :], nb[0:1, :])
+        load_scales(nc.sync, k_sc_all, k_scales)
+        nc.sync.dma_start(q_raw[:], qT[0].rearrange("(p j) q -> p j q", j=PACK))
+        k_all = load_words("k_all", k_words, "slot_d")
+        load_scales(nc.sync, c_sc_all, c_scales)
+        nc.sync.dma_start(us_col[:], us[0].rearrange("(p t) o -> p (t o)", t=PACK))
+        make_identity(nc, ident[:])
+        nc.scalar.activation(warm[:, 1:2], warm[:, 0:1], ACT.Silu)
+
+        def gather_scales(window, name):
+            listed = sbuf(name + "_listed", [P, N], U8)
+            nc.vector.tensor_copy(listed[:], window[:].indirect(offsets[:]))
+            return listed
+
+        def arrange_scales(listed, name):
+            plane = sbuf(name + "_plane", [P, PACK, P], U8)
+            nc.vector.tensor_copy(plane[:], listed[:].rearrange("p (m t) -> p t m", t=PACK))
+            return plane
+
+        def gather_words(window, name, slot):
+            codes = sbuf(name, [P, PACK, P], U32, slot)
+            nc.vector.tensor_copy(codes[:].rearrange("p t m -> p m t"), window[:].bitcast(U32).indirect(offsets[:]))
+            return codes
+
+        nb_listed = sbuf("nb_listed", [P, N], F32)
+        nc.vector.tensor_copy(nb_listed[:], nb_all[:].indirect(offsets[:]))
+        c_all = load_words("c_all", c_words, "slot_a")
+        k_listed = gather_scales(k_sc_all, "k")
+        v_all = [load_values(0, "slot_b")]
+        c_listed = gather_scales(c_sc_all, "c")
+        v_all.append(load_values(1, "slot_c"))
+        k_plane = arrange_scales(k_listed, "k")
+        c_plane = arrange_scales(c_listed, "c")
+
+        nb_ps = psum.tile([P, PACK, P], F32, name="nb_ps", tag="turn")
+        for t in range(PACK):
+            nc.tensor.transpose(nb_ps[:, t, :], nb_listed[:, t:N:PACK], ident[:])
+
+        q_bf = sbuf("q_bf", [P, NQ, PACK], BF16)
+        q_codes = sbuf("q_codes", [P, NQ], U32)
+        q_plane = sbuf("q_plane", [P, NQ], U8)
+        for cols in halves:
+            nc.scalar.copy(q_bf[:, cols, :], q_raw[:, :, cols].rearrange("p j q -> p q j"))
+        nb_col = keep.tile([P, PACK, 1], F32, name="nb_col")
+        nc.scalar.copy(nb_col[:], nb_ps[:, :, P - 1 : P])
+
+        k_codes = gather_words(k_all, "k_codes", None)
+        v_all.append(load_values(2, "slot_d"))
+        for cols in halves:
+            quantize(q_codes, q_plane, q_bf, cols)
+
+        gate = sbuf("gate", [P, PACK, NQ], F32, "slot_g")
+        for t in range(PACK):
+            a_ps = psum.tile([P, NQ], F32, name="a_ps", tag="wide")
+            matmul(a_ps[:], k_codes[:, t, :], k_plane[:, t, :], q_codes[:], q_plane[:])
+            nc.scalar.activation(gate[:, t, :], a_ps[:], ACT.Silu, bias=nb_col[:, t, :])
+
+        c_codes = gather_words(c_all, "c_codes", "slot_f")
+        v_all.append(load_values(3, "slot_a"))
+
+        y_rows = sbuf("y_rows", [P, PACK, NQ], BF16)
+        y_bf = sbuf("y_bf", [P, NQ, PACK], BF16, "slot_h")
+        y_codes = sbuf("y_codes", [P, NQ], U32)
+        y_plane = sbuf("y_plane", [P, NQ], U8)
+        for cols in halves:
+            for u in range(2):
+                z_ps = psum.tile([P, 2, HALF], F32, name="z_ps", tag="lin")
+                for h in range(2):
+                    t = 2 * u + h
+                    matmul(z_ps[:, h, :], c_codes[:, t, :], c_plane[:, t, :], q_codes[:, cols], q_plane[:, cols])
+                for h in range(2):
+                    t = 2 * u + h
+                    nc.vector.scalar_tensor_tensor(
+                        out=y_rows[:, t, cols], in0=z_ps[:, h, :], scalar=us_col[:, t : t + 1], in1=gate[:, t, cols],
+                        op0=ALU.mult, op1=ALU.mult,
+                    )
+            nc.scalar.copy(y_bf[:, cols, :], y_rows[:, :, cols].rearrange("p t q -> p q t"))
+
+        v_bf = sbuf("v_bf", [P, DV, PACK], BF16)
+        v_codes = sbuf("v_codes", [P, DV], U32)
+        v_plane = sbuf("v_plane", [P, DV], U8)
+        blocks = [slice(j * P, (j + 1) * P) for j in range(DV // P)]
+
+        def gather_values(j, slot):
+            listed = sbuf("v_listed%d" % j, [P, 2, P, 2], BF16, slot)
+            nc.vector.tensor_copy(listed[:].rearrange("e u m h -> e m u h"), v_all[j][:].indirect(offsets[:]))
+            words = listed[:].rearrange("e u m h -> e (u m h)").bitcast(F32)
+            turned = psum.tile([P, PACK, P], F32, name="v_turned", tag="turn")
+            for u in range(2):
+                nc.tensor.transpose(turned[:, u, :], words[:, u * P : (u + 1) * P], ident[:])
+            dst = v_bf[:, blocks[j], :].rearrange("p e t -> p (e t)").bitcast(F32)
+            nc.scalar.copy(dst.rearrange("p (e u) -> p e u", u=2), turned[:, 0:2, :].rearrange("p u e -> p e u"))
+
+        out_view = out[0].rearrange("(b p) e -> p b e", p=P)
+
+        def multiply(j):
+            o_ps = psum.tile([P, NQ // P, P], F32, name="o_ps", tag="wide")
+            for b in range(NQ // P):
+                rows = slice(b * P, (b + 1) * P)
+                matmul(o_ps[:, b, :], y_codes[:, rows], y_plane[:, rows], v_codes[:, blocks[j]], v_plane[:, blocks[j]])
+            res = sbuf("res%d" % j, [P, NQ // P, P], F32)
+            nc.scalar.copy(res[:], o_ps[:])
+            nc.sync.dma_start(out_view[:, :, blocks[j]], res[:])
+
+        gather_values(0, "slot_f")
+        quantize(y_codes, y_plane, y_bf, halves[0])
+        gather_values(1, "slot_g")
+        quantize(y_codes, y_plane, y_bf, halves[1])
+        quantize(v_codes, v_plane, v_bf, blocks[0])
+        gather_values(2, "slot_f")
+        quantize(v_codes, v_plane, v_bf, blocks[1])
+        multiply(0)
+        gather_values(3, "slot_h")
+        multiply(1)
+        quantize(v_codes, v_plane, v_bf, blocks[2])
+        quantize(v_codes, v_plane, v_bf, blocks[3])
+        multiply(2)
+        multiply(3)

@@ -30,6 +30,7 @@ def tile_attend_mlpb_swiglu_topk_kernel(tc, qT, k_words, k_scales, c_words, c_sc
     with ExitStack() as ctx:
         keep = ctx.enter_context(tc.tile_pool(name="keep", bufs=1))
         psum = ctx.enter_context(tc.psum_pool(name="psum", bufs=2))
+        psum4 = ctx.enter_context(tc.psum_pool(name="psum4", bufs=4))
 
         def sbuf(name, shape, dtype, slot=None):
             return keep.tile(shape, dtype, name=name, tag=slot or name, align_bytes=64)
@@ -69,26 +70,28 @@ def tile_attend_mlpb_swiglu_topk_kernel(tc, qT, k_words, k_scales, c_words, c_sc
         offsets = keep.tile([P, N // 16], U16, name="offsets")
         nc.sync.dma_start(offsets[:], offs)
 
-        k_sc_all = sbuf("k_sc_all", [P, T], U8, "slot_b")
-        c_sc_all = sbuf("c_sc_all", [P, T], U8, "slot_c")
-        nb_all = sbuf("nb_all", [P, T], F32, "slot_a")
+        k_sc_all = sbuf("k_sc_all", [P, T], U8)
+        c_sc_all = sbuf("c_sc_all", [P, T], U8)
+        nb_all = sbuf("nb_all", [P, T], F32)
         nc.gpsimd.memset(k_sc_all[:].bitcast(I32), 0)
         nc.gpsimd.memset(c_sc_all[:].bitcast(I32), 0)
-        nc.vector.memset(nb_all[0 : P - 1, :], 0.0)
         warm = keep.tile([P, 2], F32, name="warm")
         nc.vector.memset(warm[:, 0:1], 0.0)
-        q_raw = sbuf("q_raw", [P, PACK, NQ], F32)
-        us_col = keep.tile([P, PACK], F32, name="us_col")
+        nc.vector.memset(nb_all[0 : P - 1, :], 0.0)
+        nc.scalar.activation(warm[:, 1:2], warm[:, 0:1], ACT.Silu)
         ident = keep.tile([P, P], F32, name="ident")
+        make_identity(nc, ident[:])
 
+        q_raw = sbuf("q_raw", [P, PACK, NQ], F32, "slot_q")
+        us_col = sbuf("us_col", [P, PACK], F32)
         nc.sync.dma_start(nb_all[P - 1 : P, :], nb[0:1, :])
         load_scales(nc.sync, k_sc_all, k_scales)
         nc.sync.dma_start(q_raw[:], qT[0].rearrange("(p j) q -> p j q", j=PACK))
-        k_all = load_words("k_all", k_words, "slot_d")
         load_scales(nc.sync, c_sc_all, c_scales)
+        k_all = load_words("k_all", k_words, "slot_k")
         nc.sync.dma_start(us_col[:], us[0].rearrange("(p t) o -> p (t o)", t=PACK))
-        make_identity(nc, ident[:])
-        nc.scalar.activation(warm[:, 1:2], warm[:, 0:1], ACT.Silu)
+        c_all = load_words("c_all", c_words, None)
+        v_all = [load_values(j, "slot_v%d" % j) for j in range(DV // P)]
 
         def gather_scales(window, name):
             listed = sbuf(name + "_listed", [P, N], U8)
@@ -107,11 +110,8 @@ def tile_attend_mlpb_swiglu_topk_kernel(tc, qT, k_words, k_scales, c_words, c_sc
 
         nb_listed = sbuf("nb_listed", [P, N], F32)
         nc.vector.tensor_copy(nb_listed[:], nb_all[:].indirect(offsets[:]))
-        c_all = load_words("c_all", c_words, "slot_a")
         k_listed = gather_scales(k_sc_all, "k")
-        v_all = [load_values(0, "slot_b")]
         c_listed = gather_scales(c_sc_all, "c")
-        v_all.append(load_values(1, "slot_c"))
         k_plane = arrange_scales(k_listed, "k")
         c_plane = arrange_scales(c_listed, "c")
 
@@ -120,53 +120,48 @@ def tile_attend_mlpb_swiglu_topk_kernel(tc, qT, k_words, k_scales, c_words, c_sc
             nc.tensor.transpose(nb_ps[:, t, :], nb_listed[:, t:N:PACK], ident[:])
 
         q_bf = sbuf("q_bf", [P, NQ, PACK], BF16)
-        q_codes = sbuf("q_codes", [P, NQ], U32)
         q_plane = sbuf("q_plane", [P, NQ], U8)
         for cols in halves:
             nc.scalar.copy(q_bf[:, cols, :], q_raw[:, :, cols].rearrange("p j q -> p q j"))
-        nb_col = keep.tile([P, PACK, 1], F32, name="nb_col")
+        nb_col = sbuf("nb_col", [P, PACK, 1], F32, "slot_q")
         nc.scalar.copy(nb_col[:], nb_ps[:, :, P - 1 : P])
 
         k_codes = gather_words(k_all, "k_codes", None)
-        v_all.append(load_values(2, "slot_d"))
-        for cols in halves:
-            quantize(q_codes, q_plane, q_bf, cols)
+        q_codes = sbuf("q_codes", [P, NQ], U32, "slot_k")
+        quantize(q_codes, q_plane, q_bf, slice(0, NQ))
 
-        gate = sbuf("gate", [P, PACK, NQ], F32, "slot_g")
-        for t in range(PACK):
-            a_ps = psum.tile([P, NQ], F32, name="a_ps", tag="wide")
-            matmul(a_ps[:], k_codes[:, t, :], k_plane[:, t, :], q_codes[:], q_plane[:])
-            nc.scalar.activation(gate[:, t, :], a_ps[:], ACT.Silu, bias=nb_col[:, t, :])
-
-        c_codes = gather_words(c_all, "c_codes", "slot_f")
-        v_all.append(load_values(3, "slot_a"))
-
-        y_rows = sbuf("y_rows", [P, PACK, NQ], BF16)
-        y_bf = sbuf("y_bf", [P, NQ, PACK], BF16, "slot_h")
-        y_codes = sbuf("y_codes", [P, NQ], U32)
-        y_plane = sbuf("y_plane", [P, NQ], U8)
+        gate = sbuf("gate", [P, PACK, NQ], F32)
+        scaled = sbuf("scaled", [P, PACK, NQ], F32, "slot_s")
         for cols in halves:
             for u in range(2):
-                z_ps = psum.tile([P, 2, HALF], F32, name="z_ps", tag="lin")
+                a_ps = psum4.tile([P, 2, HALF], F32, name="a_ps", tag="wide")
                 for h in range(2):
                     t = 2 * u + h
-                    matmul(z_ps[:, h, :], c_codes[:, t, :], c_plane[:, t, :], q_codes[:, cols], q_plane[:, cols])
+                    matmul(a_ps[:, h, :], k_codes[:, t, :], k_plane[:, t, :], q_codes[:, cols], q_plane[:, cols])
                 for h in range(2):
                     t = 2 * u + h
-                    nc.vector.scalar_tensor_tensor(
-                        out=y_rows[:, t, cols], in0=z_ps[:, h, :], scalar=us_col[:, t : t + 1], in1=gate[:, t, cols],
-                        op0=ALU.mult, op1=ALU.mult,
+                    nc.scalar.activation(gate[:, t, cols], a_ps[:, h, :], ACT.Silu, bias=nb_col[:, t, :])
+                    nc.gpsimd.tensor_scalar(
+                        out=scaled[:, t, cols], in0=gate[:, t, cols], scalar1=us_col[:, t : t + 1], scalar2=0.0,
+                        op0=ALU.mult, op1=ALU.add,
                     )
-            nc.scalar.copy(y_bf[:, cols, :], y_rows[:, :, cols].rearrange("p t q -> p q t"))
 
-        v_bf = sbuf("v_bf", [P, DV, PACK], BF16)
-        v_codes = sbuf("v_codes", [P, DV], U32)
-        v_plane = sbuf("v_plane", [P, DV], U8)
+        c_codes = gather_words(c_all, "c_codes", None)
+
         blocks = [slice(j * P, (j + 1) * P) for j in range(DV // P)]
+        v_bf = sbuf("v_bf", [P, DV, PACK], BF16)
+        v_plane = sbuf("v_plane", [P, DV], U8)
+        v_codes = {}
 
-        def gather_values(j, slot):
-            listed = sbuf("v_listed%d" % j, [P, 2, P, 2], BF16, slot)
-            nc.vector.tensor_copy(listed[:].rearrange("e u m h -> e m u h"), v_all[j][:].indirect(offsets[:]))
+        def gather_values(j, on_scalar):
+            listed = sbuf("v_listed%d" % j, [P, 2, P, 2], BF16)
+            by_slot = listed[:].rearrange("e u m h -> e m u h")
+            if on_scalar:
+                rounded = sbuf("v_rounded%d" % j, [P, T], BF16)
+                nc.scalar.activation(rounded[:], v_all[j][:], ACT.Copy)
+                nc.scalar.activation(by_slot, rounded[:].indirect(offsets[:]), ACT.Copy)
+            else:
+                nc.vector.tensor_copy(by_slot, v_all[j][:].indirect(offsets[:]))
             words = listed[:].rearrange("e u m h -> e (u m h)").bitcast(F32)
             turned = psum.tile([P, PACK, P], F32, name="v_turned", tag="turn")
             for u in range(2):
@@ -174,28 +169,61 @@ def tile_attend_mlpb_swiglu_topk_kernel(tc, qT, k_words, k_scales, c_words, c_sc
             dst = v_bf[:, blocks[j], :].rearrange("p e t -> p (e t)").bitcast(F32)
             nc.scalar.copy(dst.rearrange("p (e u) -> p e u", u=2), turned[:, 0:2, :].rearrange("p u e -> p e u"))
 
+        def quantize_values(j, slot):
+            v_codes[j] = sbuf("v_codes%d" % j, [P, P], U32, slot)
+            nc.vector.quantize_mx(
+                out=v_codes[j][:].bitcast(FP8X4),
+                scales=v_plane[:, blocks[j]],
+                in_=v_bf[:, blocks[j], :].rearrange("p c t -> p (c t)"),
+            )
+
         out_view = out[0].rearrange("(b p) e -> p b e", p=P)
 
-        def multiply(j):
-            o_ps = psum.tile([P, NQ // P, P], F32, name="o_ps", tag="wide")
+        def multiply(j, slot):
+            o_ps = psum4.tile([P, NQ // P, P], F32, name="o_ps", tag="wide")
             for b in range(NQ // P):
                 rows = slice(b * P, (b + 1) * P)
-                matmul(o_ps[:, b, :], y_codes[:, rows], y_plane[:, rows], v_codes[:, blocks[j]], v_plane[:, blocks[j]])
-            res = sbuf("res%d" % j, [P, NQ // P, P], F32)
+                matmul(o_ps[:, b, :], y_codes[:, rows], y_plane[:, rows], v_codes[j][:], v_plane[:, blocks[j]])
+            res = sbuf("res%d" % j, [P, NQ // P, P], F32, slot)
             nc.scalar.copy(res[:], o_ps[:])
             nc.sync.dma_start(out_view[:, :, blocks[j]], res[:])
 
-        gather_values(0, "slot_f")
+        def multiply_last(j):
+            for pair in range(2):
+                o_ps = psum.tile([P, 2, P], F32, name="o_last", tag="lin")
+                for b in range(2):
+                    rows = blocks[2 * pair + b]
+                    matmul(o_ps[:, b, :], y_codes[:, rows], y_plane[:, rows], v_codes[j][:], v_plane[:, blocks[j]])
+                res = sbuf("res_last%d" % pair, [P, 2, P], F32)
+                if pair == 0:
+                    nc.scalar.copy(res[:], o_ps[:])
+                else:
+                    nc.vector.tensor_copy(res[:], o_ps[:])
+                nc.sync.dma_start(out_view[:, 2 * pair : 2 * pair + 2, blocks[j]], res[:])
+
+        gather_values(0, False)
+
+        y_bf = sbuf("y_bf", [P, NQ, PACK], BF16, "slot_v0")
+        y_codes = sbuf("y_codes", [P, NQ], U32)
+        y_plane = sbuf("y_plane", [P, NQ], U8)
+        for cols in blocks:
+            z_ps = psum.tile([P, PACK, P], F32, name="z_ps", tag="lin")
+            for t in range(PACK):
+                matmul(z_ps[:, t, :], c_codes[:, t, :], c_plane[:, t, :], q_codes[:, cols], q_plane[:, cols])
+            nc.vector.tensor_tensor(
+                y_bf[:, cols, :], z_ps[:].rearrange("p t q -> p q t"), scaled[:, :, cols].rearrange("p t q -> p q t"), ALU.mult
+            )
+
         quantize(y_codes, y_plane, y_bf, halves[0])
-        gather_values(1, "slot_g")
         quantize(y_codes, y_plane, y_bf, halves[1])
-        quantize(v_codes, v_plane, v_bf, blocks[0])
-        gather_values(2, "slot_f")
-        quantize(v_codes, v_plane, v_bf, blocks[1])
-        multiply(0)
-        gather_values(3, "slot_h")
-        multiply(1)
-        quantize(v_codes, v_plane, v_bf, blocks[2])
-        quantize(v_codes, v_plane, v_bf, blocks[3])
-        multiply(2)
-        multiply(3)
+        gather_values(1, True)
+        quantize_values(0, "slot_s")
+        gather_values(2, False)
+        quantize_values(1, "slot_v2")
+        multiply(0, "slot_v1")
+        gather_values(3, False)
+        multiply(1, None)
+        quantize_values(2, "slot_v3")
+        quantize_values(3, None)
+        multiply(2, None)
+        multiply_last(3)

@@ -21,6 +21,7 @@ NQ = 512
 D = 512
 DV = 512
 HALF = NQ // 2
+C_ROW = 4
 FLOPS = 2 * N * NQ * (2 * D + DV)
 BYTES = 4 * D * NQ + 2 * (D * T + D * T // 32) + 4 * DV * T + 4 * T + 4 * N + 2 * N + 4 * NQ * DV
 
@@ -35,12 +36,9 @@ def tile_attend_mlpb_swiglu_topk_kernel(tc, qT, k_words, k_scales, c_words, c_sc
         def sbuf(name, shape, dtype, slot=None):
             return keep.tile(shape, dtype, name=name, tag=slot or name, align_bytes=64)
 
-        def load_scales(queue, tile, scales):
-            for quad in range(4):
-                queue.dma_start(
-                    tile[32 * quad : 32 * quad + 4, :].bitcast(I32),
-                    scales[0, 4 * quad : 4 * quad + 4, :].bitcast(I32),
-                )
+        def load_scales(tile, scales, first):
+            for r in range(4):
+                nc.sync.dma_start(tile[first + r : P : 32, :].bitcast(I32), scales[0, r:16:4, :].bitcast(I32))
 
         def load_words(name, words, slot):
             tile = sbuf(name, [P, T], I32, slot)
@@ -70,14 +68,14 @@ def tile_attend_mlpb_swiglu_topk_kernel(tc, qT, k_words, k_scales, c_words, c_sc
         offsets = keep.tile([P, N // 16], U16, name="offsets")
         nc.sync.dma_start(offsets[:], offs)
 
-        k_sc_all = sbuf("k_sc_all", [P, T], U8)
+        k_sc_all = sbuf("k_sc_all", [P, T], U8, "slot_s0")
         c_sc_all = sbuf("c_sc_all", [P, T], U8)
         nb_all = sbuf("nb_all", [P, T], F32)
-        nc.gpsimd.memset(k_sc_all[:].bitcast(I32), 0)
-        nc.gpsimd.memset(c_sc_all[:].bitcast(I32), 0)
         warm = keep.tile([P, 2], F32, name="warm")
+        nc.vector.memset(k_sc_all[:].bitcast(I32), 0)
         nc.vector.memset(warm[:, 0:1], 0.0)
         nc.vector.memset(nb_all[0 : P - 1, :], 0.0)
+        nc.vector.memset(c_sc_all[:].bitcast(I32), 0)
         nc.scalar.activation(warm[:, 1:2], warm[:, 0:1], ACT.Silu)
         ident = keep.tile([P, P], F32, name="ident")
         make_identity(nc, ident[:])
@@ -85,10 +83,10 @@ def tile_attend_mlpb_swiglu_topk_kernel(tc, qT, k_words, k_scales, c_words, c_sc
         q_raw = sbuf("q_raw", [P, PACK, NQ], F32, "slot_q")
         us_col = sbuf("us_col", [P, PACK], F32)
         nc.sync.dma_start(nb_all[P - 1 : P, :], nb[0:1, :])
-        load_scales(nc.sync, k_sc_all, k_scales)
         nc.sync.dma_start(q_raw[:], qT[0].rearrange("(p j) q -> p j q", j=PACK))
-        load_scales(nc.sync, c_sc_all, c_scales)
+        load_scales(k_sc_all, k_scales, 0)
         k_all = load_words("k_all", k_words, "slot_k")
+        load_scales(c_sc_all, c_scales, C_ROW)
         nc.sync.dma_start(us_col[:], us[0].rearrange("(p t) o -> p (t o)", t=PACK))
         c_all = load_words("c_all", c_words, None)
         v_all = [load_values(j, "slot_v%d" % j) for j in range(DV // P)]
@@ -111,9 +109,7 @@ def tile_attend_mlpb_swiglu_topk_kernel(tc, qT, k_words, k_scales, c_words, c_sc
         nb_listed = sbuf("nb_listed", [P, N], F32)
         nc.vector.tensor_copy(nb_listed[:], nb_all[:].indirect(offsets[:]))
         k_listed = gather_scales(k_sc_all, "k")
-        c_listed = gather_scales(c_sc_all, "c")
         k_plane = arrange_scales(k_listed, "k")
-        c_plane = arrange_scales(c_listed, "c")
 
         nb_ps = psum.tile([P, PACK, P], F32, name="nb_ps", tag="turn")
         for t in range(PACK):
@@ -126,18 +122,29 @@ def tile_attend_mlpb_swiglu_topk_kernel(tc, qT, k_words, k_scales, c_words, c_sc
         nb_col = sbuf("nb_col", [P, PACK, 1], F32, "slot_q")
         nc.scalar.copy(nb_col[:], nb_ps[:, :, P - 1 : P])
 
+        def quantize_queries(h, slot):
+            codes = sbuf("q_codes%d" % h, [P, HALF], U32, slot)
+            nc.vector.quantize_mx(
+                out=codes[:].bitcast(FP8X4),
+                scales=q_plane[:, halves[h]],
+                in_=q_bf[:, halves[h], :].rearrange("p c t -> p (c t)"),
+            )
+            return codes
+
+        q_codes = [quantize_queries(0, "slot_s0")]
         k_codes = gather_words(k_all, "k_codes", None)
-        q_codes = sbuf("q_codes", [P, NQ], U32, "slot_k")
-        quantize(q_codes, q_plane, q_bf, slice(0, NQ))
+        q_codes.append(quantize_queries(1, "slot_k"))
+        c_listed = gather_scales(c_sc_all, "c")
+        c_plane = arrange_scales(c_listed, "c")
 
         gate = sbuf("gate", [P, PACK, NQ], F32)
         scaled = sbuf("scaled", [P, PACK, NQ], F32, "slot_s")
-        for cols in halves:
+        for g, cols in enumerate(halves):
             for u in range(2):
                 a_ps = psum4.tile([P, 2, HALF], F32, name="a_ps", tag="wide")
                 for h in range(2):
                     t = 2 * u + h
-                    matmul(a_ps[:, h, :], k_codes[:, t, :], k_plane[:, t, :], q_codes[:, cols], q_plane[:, cols])
+                    matmul(a_ps[:, h, :], k_codes[:, t, :], k_plane[:, t, :], q_codes[g][:], q_plane[:, cols])
                 for h in range(2):
                     t = 2 * u + h
                     nc.scalar.activation(gate[:, t, cols], a_ps[:, h, :], ACT.Silu, bias=nb_col[:, t, :])
@@ -206,10 +213,10 @@ def tile_attend_mlpb_swiglu_topk_kernel(tc, qT, k_words, k_scales, c_words, c_sc
         y_bf = sbuf("y_bf", [P, NQ, PACK], BF16, "slot_v0")
         y_codes = sbuf("y_codes", [P, NQ], U32)
         y_plane = sbuf("y_plane", [P, NQ], U8)
-        for cols in blocks:
+        for b, cols in enumerate(blocks):
             z_ps = psum.tile([P, PACK, P], F32, name="z_ps", tag="lin")
             for t in range(PACK):
-                matmul(z_ps[:, t, :], c_codes[:, t, :], c_plane[:, t, :], q_codes[:, cols], q_plane[:, cols])
+                matmul(z_ps[:, t, :], c_codes[:, t, :], c_plane[C_ROW:P, t, :], q_codes[b // 2][:, blocks[b % 2]], q_plane[:, cols])
             nc.vector.tensor_tensor(
                 y_bf[:, cols, :], z_ps[:].rearrange("p t q -> p q t"), scaled[:, :, cols].rearrange("p t q -> p q t"), ALU.mult
             )

@@ -15,6 +15,7 @@ ALU = mybir.AluOpType
 
 P = 128
 PACK = 4
+RUN = 4
 T = 2048
 N = 512
 NQ = 512
@@ -30,32 +31,30 @@ def tile_attend_mlpb_swiglu_topk_kernel(tc, qT, k_words, k_scales, c_words, c_sc
     nc = tc.nc
     with ExitStack() as ctx:
         keep = ctx.enter_context(tc.tile_pool(name="keep", bufs=1))
-        psum = ctx.enter_context(tc.psum_pool(name="psum", bufs=2))
-        psum4 = ctx.enter_context(tc.psum_pool(name="psum4", bufs=4))
+        psum = ctx.enter_context(tc.psum_pool(name="psum", bufs=1))
 
         def sbuf(name, shape, dtype, slot=None):
             return keep.tile(shape, dtype, name=name, tag=slot or name, align_bytes=64)
 
-        def load_scales(tile, scales, first):
-            for r in range(4):
-                nc.sync.dma_start(tile[first + r : P : 32, :].bitcast(I32), scales[0, r:16:4, :].bitcast(I32))
+        def bank(index, shape, name):
+            return psum.tile(shape, F32, name=name, tag="bank%d" % index)
 
-        def load_words(name, words, slot):
-            tile = sbuf(name, [P, T], I32, slot)
+        def load_scales(queue, tile, scales, first):
+            for r in range(4):
+                queue.dma_start(tile[first + r : P : 32, :].bitcast(I32), scales[0, r:16:4, :].bitcast(I32))
+
+        def load_words(name, words):
+            tile = sbuf(name, [P, T], I32, "slot_" + name)
             nc.sync.dma_start(tile[:], words[0].rearrange("p t r -> p (t r)").bitcast(I32))
             return tile
 
-        def load_values(j, slot):
-            tile = sbuf("v_all%d" % j, [P, T], F32, slot)
+        def load_values(j):
+            tile = sbuf("v_all%d" % j, [P, T], F32, "slot_v%d" % j)
             nc.sync.dma_start(tile[:], vT[j * P : (j + 1) * P, :])
             return tile
 
-        def quantize(codes, plane, values, cols):
-            nc.vector.quantize_mx(
-                out=codes[:, cols].bitcast(FP8X4),
-                scales=plane[:, cols],
-                in_=values[:, cols, :].rearrange("p c t -> p (c t)"),
-            )
+        def quantize(codes, plane, values):
+            nc.vector.quantize_mx(out=codes.bitcast(FP8X4), scales=plane, in_=values.rearrange("p c t -> p (c t)"))
 
         def matmul(acc, lhs_codes, lhs_plane, rhs_codes, rhs_plane):
             nc.tensor.matmul_mx(
@@ -63,7 +62,11 @@ def tile_attend_mlpb_swiglu_topk_kernel(tc, qT, k_words, k_scales, c_words, c_sc
                 rhs=rhs_codes.bitcast(FP8X4), rhs_scale=rhs_plane, start=True, stop=True,
             )
 
+        def interleave(dst, src):
+            nc.scalar.copy(dst.rearrange("p (c i) t -> p c t i", i=RUN), src.rearrange("p t (c i) -> p c t i", i=RUN))
+
         halves = [slice(h * HALF, (h + 1) * HALF) for h in range(2)]
+        blocks = [slice(j * P, (j + 1) * P) for j in range(DV // P)]
 
         offsets = keep.tile([P, N // 16], U16, name="offsets")
         nc.sync.dma_start(offsets[:], offs)
@@ -71,166 +74,147 @@ def tile_attend_mlpb_swiglu_topk_kernel(tc, qT, k_words, k_scales, c_words, c_sc
         k_sc_all = sbuf("k_sc_all", [P, T], U8, "slot_s0")
         c_sc_all = sbuf("c_sc_all", [P, T], U8)
         nb_all = sbuf("nb_all", [P, T], F32)
+        us_rows = sbuf("us_rows", [P, P], F32)
         warm = keep.tile([P, 2], F32, name="warm")
         nc.vector.memset(k_sc_all[:].bitcast(I32), 0)
-        nc.vector.memset(warm[:, 0:1], 0.0)
-        nc.vector.memset(nb_all[0 : P - 1, :], 0.0)
         nc.vector.memset(c_sc_all[:].bitcast(I32), 0)
-        nc.scalar.activation(warm[:, 1:2], warm[:, 0:1], ACT.Silu)
+        nc.vector.memset(warm[:, 0:1], 0.0)
+        nc.vector.memset(nb_all[0 : P - 1, 0 : T // 2], 0.0)
+        nc.vector.memset(us_rows[0 : P - PACK, :], 0.0)
         ident = keep.tile([P, P], F32, name="ident")
         make_identity(nc, ident[:])
+        nc.gpsimd.memset(nb_all[0 : P - 1, T // 2 : T], 0.0)
 
-        q_raw = sbuf("q_raw", [P, PACK, NQ], F32, "slot_q")
-        us_col = sbuf("us_col", [P, PACK], F32)
+        q_view = qT[0].rearrange("(p j) q -> p j q", j=PACK)
+
+        def load_queries(g):
+            tile = sbuf("q_raw%d" % g, [P, PACK, HALF], F32, "slot_q%d" % g)
+            nc.sync.dma_start(tile[:], q_view[:, :, halves[g]])
+            return tile
+
         nc.sync.dma_start(nb_all[P - 1 : P, :], nb[0:1, :])
-        nc.sync.dma_start(q_raw[:], qT[0].rearrange("(p j) q -> p j q", j=PACK))
-        load_scales(k_sc_all, k_scales, 0)
-        k_all = load_words("k_all", k_words, "slot_k")
-        load_scales(c_sc_all, c_scales, C_ROW)
-        nc.sync.dma_start(us_col[:], us[0].rearrange("(p t) o -> p (t o)", t=PACK))
-        c_all = load_words("c_all", c_words, None)
-        v_all = [load_values(j, "slot_v%d" % j) for j in range(DV // P)]
+        q_raw = [load_queries(0)]
+        load_scales(nc.sync, k_sc_all, k_scales, 0)
+        nc.scalar.activation(warm[:, 1:2], warm[:, 0:1], ACT.Silu)
+        k_all = load_words("k_all", k_words)
+        load_scales(nc.sync, c_sc_all, c_scales, C_ROW)
+        q_raw.append(load_queries(1))
+        nc.sync.dma_start(
+            us_rows[P - PACK : P, :].rearrange("t (m b) -> t m b", b=RUN),
+            us[0].rearrange("(m t b) o -> t m (b o)", t=PACK, b=RUN),
+        )
+        c_all = load_words("c_all", c_words)
+        v_all = [load_values(j) for j in range(DV // P)]
 
         def gather_scales(window, name):
             listed = sbuf(name + "_listed", [P, N], U8)
             nc.vector.tensor_copy(listed[:], window[:].indirect(offsets[:]))
-            return listed
-
-        def arrange_scales(listed, name):
             plane = sbuf(name + "_plane", [P, PACK, P], U8)
-            nc.vector.tensor_copy(plane[:], listed[:].rearrange("p (m t) -> p t m", t=PACK))
+            nc.vector.tensor_copy(
+                plane[:].rearrange("p t m -> p (t m)").bitcast(I32).rearrange("p (t m) -> p t m", t=PACK),
+                listed[:].bitcast(I32).rearrange("p (m t) -> p t m", t=PACK),
+            )
             return plane
 
-        def gather_words(window, name, slot):
-            codes = sbuf(name, [P, PACK, P], U32, slot)
-            nc.vector.tensor_copy(codes[:].rearrange("p t m -> p m t"), window[:].bitcast(U32).indirect(offsets[:]))
-            return codes
+        def gather_words(window, name, dtype):
+            words = sbuf(name, [P, PACK, P], dtype)
+            nc.vector.tensor_copy(
+                words[:].bitcast(U32).rearrange("p t (m b) -> p m t b", b=RUN), window[:].bitcast(U32).indirect(offsets[:])
+            )
+            return words
 
-        nb_listed = sbuf("nb_listed", [P, N], F32)
-        nc.vector.tensor_copy(nb_listed[:], nb_all[:].indirect(offsets[:]))
-        k_listed = gather_scales(k_sc_all, "k")
-        k_plane = arrange_scales(k_listed, "k")
+        nb_listed = gather_words(nb_all, "nb_listed", F32)
+        k_plane = gather_scales(k_sc_all, "k")
 
-        nb_ps = psum.tile([P, PACK, P], F32, name="nb_ps", tag="turn")
+        nb_ps = bank(4, [P, PACK, P], "nb_ps")
         for t in range(PACK):
-            nc.tensor.transpose(nb_ps[:, t, :], nb_listed[:, t:N:PACK], ident[:])
+            nc.tensor.transpose(nb_ps[:, t, :], nb_listed[:, t, :], ident[:])
+        us_ps = bank(5, [P, P], "us_ps")
+        nc.tensor.transpose(us_ps[:], us_rows[:], ident[:])
 
         q_bf = sbuf("q_bf", [P, NQ, PACK], BF16)
         q_plane = sbuf("q_plane", [P, NQ], U8)
-        for cols in halves:
-            nc.scalar.copy(q_bf[:, cols, :], q_raw[:, :, cols].rearrange("p j q -> p q j"))
-        nb_col = sbuf("nb_col", [P, PACK, 1], F32, "slot_q")
+        for g, cols in enumerate(halves):
+            interleave(q_bf[:, cols, :], q_raw[g][:])
+        nb_col = sbuf("nb_col", [P, PACK, 1], F32, "slot_q0")
         nc.scalar.copy(nb_col[:], nb_ps[:, :, P - 1 : P])
+        us_col = sbuf("us_col", [P, PACK], F32)
+        nc.scalar.copy(us_col[:], us_ps[:, P - PACK : P])
 
-        def quantize_queries(h, slot):
-            codes = sbuf("q_codes%d" % h, [P, HALF], U32, slot)
-            nc.vector.quantize_mx(
-                out=codes[:].bitcast(FP8X4),
-                scales=q_plane[:, halves[h]],
-                in_=q_bf[:, halves[h], :].rearrange("p c t -> p (c t)"),
-            )
-            return codes
+        q_codes = [sbuf("q_codes0", [P, HALF], U32, "slot_s0")]
+        quantize(q_codes[0][:], q_plane[:, halves[0]], q_bf[:, halves[0], :])
+        k_codes = gather_words(k_all, "k_codes", U32)
+        c_plane = gather_scales(c_sc_all, "c")
+        q_codes.append(sbuf("q_codes1", [P, HALF], U32))
+        quantize(q_codes[1][:], q_plane[:, halves[1]], q_bf[:, halves[1], :])
 
-        q_codes = [quantize_queries(0, "slot_s0")]
-        k_codes = gather_words(k_all, "k_codes", None)
-        q_codes.append(quantize_queries(1, "slot_k"))
-        c_listed = gather_scales(c_sc_all, "c")
-        c_plane = arrange_scales(c_listed, "c")
+
+        def scores(codes, plane, t, index, name):
+            acc = bank(index, [P, 2, HALF], name)
+            for g, cols in enumerate(halves):
+                matmul(acc[:, g, :], codes[:, t, :], plane, q_codes[g][:], q_plane[:, cols])
+            return acc[:].rearrange("p g q -> p (g q)")
 
         gate = sbuf("gate", [P, PACK, NQ], F32)
-        scaled = sbuf("scaled", [P, PACK, NQ], F32, "slot_s")
-        for g, cols in enumerate(halves):
-            for u in range(2):
-                a_ps = psum4.tile([P, 2, HALF], F32, name="a_ps", tag="wide")
-                for h in range(2):
-                    t = 2 * u + h
-                    matmul(a_ps[:, h, :], k_codes[:, t, :], k_plane[:, t, :], q_codes[g][:], q_plane[:, cols])
-                for h in range(2):
-                    t = 2 * u + h
-                    nc.scalar.activation(gate[:, t, cols], a_ps[:, h, :], ACT.Silu, bias=nb_col[:, t, :])
-                    nc.gpsimd.tensor_scalar(
-                        out=scaled[:, t, cols], in0=gate[:, t, cols], scalar1=us_col[:, t : t + 1], scalar2=0.0,
-                        op0=ALU.mult, op1=ALU.add,
-                    )
+        for t in range(PACK):
+            a_ps = scores(k_codes, k_plane[:, t, :], t, t, "a_ps")
+            nc.scalar.activation(gate[:, t, :], a_ps, ACT.Silu, bias=nb_col[:, t, :])
 
-        c_codes = gather_words(c_all, "c_codes", None)
+        c_codes = gather_words(c_all, "c_codes", U32)
 
-        blocks = [slice(j * P, (j + 1) * P) for j in range(DV // P)]
+        y_rows = sbuf("y_rows", [P, PACK, NQ], BF16)
+        y_bf = sbuf("y_bf", [P, NQ, PACK], BF16)
+        y_codes = sbuf("y_codes", [P, NQ], U32)
+        y_plane = sbuf("y_plane", [P, NQ], U8)
+        for t in range(PACK):
+            z_ps = scores(c_codes, c_plane[C_ROW:P, t, :], t, PACK + t, "z_ps")
+            nc.vector.scalar_tensor_tensor(y_rows[:, t, :], z_ps, us_col[:, t : t + 1], gate[:, t, :], ALU.mult, ALU.mult)
+        for cols in halves:
+            interleave(y_bf[:, cols, :], y_rows[:, :, cols])
+
         v_bf = sbuf("v_bf", [P, DV, PACK], BF16)
         v_plane = sbuf("v_plane", [P, DV], U8)
-        v_codes = {}
 
-        def gather_values(j, on_scalar):
+        def gather_values(j):
             listed = sbuf("v_listed%d" % j, [P, 2, P, 2], BF16)
-            by_slot = listed[:].rearrange("e u m h -> e m u h")
-            if on_scalar:
-                rounded = sbuf("v_rounded%d" % j, [P, T], BF16)
-                nc.scalar.activation(rounded[:], v_all[j][:], ACT.Copy)
-                nc.scalar.activation(by_slot, rounded[:].indirect(offsets[:]), ACT.Copy)
-            else:
-                nc.vector.tensor_copy(by_slot, v_all[j][:].indirect(offsets[:]))
+            nc.vector.tensor_copy(listed[:].rearrange("e u (m b) h -> e m u h b", b=RUN), v_all[j][:].indirect(offsets[:]))
             words = listed[:].rearrange("e u m h -> e (u m h)").bitcast(F32)
-            turned = psum.tile([P, PACK, P], F32, name="v_turned", tag="turn")
+            turned = bank(j, [P, 2, P], "v_turned")
             for u in range(2):
                 nc.tensor.transpose(turned[:, u, :], words[:, u * P : (u + 1) * P], ident[:])
             dst = v_bf[:, blocks[j], :].rearrange("p e t -> p (e t)").bitcast(F32)
-            nc.scalar.copy(dst.rearrange("p (e u) -> p e u", u=2), turned[:, 0:2, :].rearrange("p u e -> p e u"))
+            nc.scalar.copy(dst.rearrange("p (e u) -> p e u", u=2), turned[:].rearrange("p u e -> p e u"))
 
-        def quantize_values(j, slot):
-            v_codes[j] = sbuf("v_codes%d" % j, [P, P], U32, slot)
-            nc.vector.quantize_mx(
-                out=v_codes[j][:].bitcast(FP8X4),
-                scales=v_plane[:, blocks[j]],
-                in_=v_bf[:, blocks[j], :].rearrange("p c t -> p (c t)"),
-            )
+        def quantize_values(cols, slot):
+            codes = sbuf("v_codes%d" % cols.start, [P, cols.stop - cols.start], U32, slot)
+            quantize(codes[:], v_plane[:, cols], v_bf[:, cols, :])
+            return codes
 
         out_view = out[0].rearrange("(b p) e -> p b e", p=P)
 
-        def multiply(j, slot):
-            o_ps = psum4.tile([P, NQ // P, P], F32, name="o_ps", tag="wide")
-            for b in range(NQ // P):
-                rows = slice(b * P, (b + 1) * P)
-                matmul(o_ps[:, b, :], y_codes[:, rows], y_plane[:, rows], v_codes[j][:], v_plane[:, blocks[j]])
-            res = sbuf("res%d" % j, [P, NQ // P, P], F32, slot)
-            nc.scalar.copy(res[:], o_ps[:])
-            nc.sync.dma_start(out_view[:, :, blocks[j]], res[:])
+        def multiply(cols, codes, rows, index, engine_copy):
+            width = cols.stop - cols.start
+            count = rows.stop - rows.start
+            o_ps = bank(index, [P, count, width], "o_ps")
+            for b in range(count):
+                block = blocks[rows.start + b]
+                matmul(o_ps[:, b, :], y_codes[:, block], y_plane[:, block], codes[:], v_plane[:, cols])
+            res = sbuf("res%d_%d" % (cols.start, rows.start), [P, count, width], F32)
+            engine_copy(res[:], o_ps[:])
+            nc.sync.dma_start(out_view[:, rows, cols], res[:])
 
-        def multiply_last(j):
-            for pair in range(2):
-                o_ps = psum.tile([P, 2, P], F32, name="o_last", tag="lin")
-                for b in range(2):
-                    rows = blocks[2 * pair + b]
-                    matmul(o_ps[:, b, :], y_codes[:, rows], y_plane[:, rows], v_codes[j][:], v_plane[:, blocks[j]])
-                res = sbuf("res_last%d" % pair, [P, 2, P], F32)
-                if pair == 0:
-                    nc.scalar.copy(res[:], o_ps[:])
-                else:
-                    nc.vector.tensor_copy(res[:], o_ps[:])
-                nc.sync.dma_start(out_view[:, 2 * pair : 2 * pair + 2, blocks[j]], res[:])
-
-        gather_values(0, False)
-
-        y_bf = sbuf("y_bf", [P, NQ, PACK], BF16, "slot_v0")
-        y_codes = sbuf("y_codes", [P, NQ], U32)
-        y_plane = sbuf("y_plane", [P, NQ], U8)
-        for b, cols in enumerate(blocks):
-            z_ps = psum.tile([P, PACK, P], F32, name="z_ps", tag="lin")
-            for t in range(PACK):
-                matmul(z_ps[:, t, :], c_codes[:, t, :], c_plane[C_ROW:P, t, :], q_codes[b // 2][:, blocks[b % 2]], q_plane[:, cols])
-            nc.vector.tensor_tensor(
-                y_bf[:, cols, :], z_ps[:].rearrange("p t q -> p q t"), scaled[:, :, cols].rearrange("p t q -> p q t"), ALU.mult
-            )
-
-        quantize(y_codes, y_plane, y_bf, halves[0])
-        quantize(y_codes, y_plane, y_bf, halves[1])
-        gather_values(1, True)
-        quantize_values(0, "slot_s")
-        gather_values(2, False)
-        quantize_values(1, "slot_v2")
-        multiply(0, "slot_v1")
-        gather_values(3, False)
-        multiply(1, None)
-        quantize_values(2, "slot_v3")
-        quantize_values(3, None)
-        multiply(2, None)
-        multiply_last(3)
+        gather_values(0)
+        quantize(y_codes[:, halves[0]], y_plane[:, halves[0]], y_bf[:, halves[0], :])
+        gather_values(1)
+        quantize(y_codes[:, halves[1]], y_plane[:, halves[1]], y_bf[:, halves[1], :])
+        gather_values(2)
+        first = slice(0, 2 * P)
+        codes = quantize_values(first, "slot_v2")
+        gather_values(3)
+        multiply(first, codes, slice(0, 2), 4, nc.scalar.copy)
+        multiply(first, codes, slice(2, 4), 5, nc.scalar.copy)
+        codes2 = quantize_values(blocks[2], "slot_v3")
+        codes3 = quantize_values(blocks[3], None)
+        multiply(blocks[2], codes2, slice(0, 4), 6, nc.vector.tensor_copy)
+        multiply(blocks[3], codes3, slice(0, 2), 7, nc.scalar.copy)
+        multiply(blocks[3], codes3, slice(2, 4), 0, nc.vector.tensor_copy)

@@ -22,7 +22,7 @@ NQ = 512
 D = 512
 DV = 512
 HALF = NQ // 2
-C_ROW = 4
+ROWS = 16
 FLOPS = 2 * N * NQ * (2 * D + DV)
 BYTES = 4 * D * NQ + 2 * (D * T + D * T // 32) + 4 * DV * T + 4 * T + 4 * N + 2 * N + 4 * NQ * DV
 
@@ -39,12 +39,11 @@ def tile_attend_mlpb_swiglu_topk_kernel(tc, qT, k_words, k_scales, c_words, c_sc
         def bank(index, shape, name):
             return psum.tile(shape, F32, name=name, tag="bank%d" % index)
 
-        def load_scales(queue, tile, scales, first):
-            for r in range(4):
-                queue.dma_start(tile[first + r : P : 32, :].bitcast(I32), scales[0, r:16:4, :].bitcast(I32))
+        def load_scales(tile, scales):
+            nc.sync.dma_start(tile[P - ROWS : P, :].bitcast(I32), scales[0].bitcast(I32))
 
-        def load_words(name, words):
-            tile = sbuf(name, [P, T], I32, "slot_" + name)
+        def load_words(name, words, slot=None):
+            tile = sbuf(name, [P, T], I32, slot)
             nc.sync.dma_start(tile[:], words[0].rearrange("p t r -> p (t r)").bitcast(I32))
             return tile
 
@@ -65,22 +64,27 @@ def tile_attend_mlpb_swiglu_topk_kernel(tc, qT, k_words, k_scales, c_words, c_sc
         def interleave(dst, src):
             nc.scalar.copy(dst.rearrange("p (c i) t -> p c t i", i=RUN), src.rearrange("p t (c i) -> p c t i", i=RUN))
 
+        def interleave_on_gpsimd(dst, src):
+            nc.gpsimd.tensor_scalar(
+                out=dst, in0=src.rearrange("p t c -> p c t"), scalar1=1.0, scalar2=0.0, op0=ALU.mult, op1=ALU.add
+            )
+
         halves = [slice(h * HALF, (h + 1) * HALF) for h in range(2)]
         blocks = [slice(j * P, (j + 1) * P) for j in range(DV // P)]
 
         offsets = keep.tile([P, N // 16], U16, name="offsets")
         nc.sync.dma_start(offsets[:], offs)
 
-        k_sc_all = sbuf("k_sc_all", [P, T], U8, "slot_s0")
-        c_sc_all = sbuf("c_sc_all", [P, T], U8)
-        nb_all = sbuf("nb_all", [P, T], F32)
-        us_rows = sbuf("us_rows", [P, P], F32)
+        k_sc_all = sbuf("k_sc_all", [P, T], U8)
+        c_sc_all = sbuf("c_sc_all", [P, T], U8, "slot_s0")
+        nb_all = sbuf("nb_all", [P, T], F32, "slot_v2")
+        us_row = sbuf("us_row", [P, N], F32)
         warm = keep.tile([P, 2], F32, name="warm")
-        nc.vector.memset(k_sc_all[:].bitcast(I32), 0)
-        nc.vector.memset(c_sc_all[:].bitcast(I32), 0)
+        nc.vector.memset(k_sc_all[0 : P - ROWS, :].bitcast(I32), 0)
+        nc.vector.memset(c_sc_all[0 : P - ROWS, :].bitcast(I32), 0)
         nc.vector.memset(warm[:, 0:1], 0.0)
         nc.vector.memset(nb_all[0 : P - 1, 0 : T // 2], 0.0)
-        nc.vector.memset(us_rows[0 : P - PACK, :], 0.0)
+        nc.gpsimd.memset(us_row[0 : P - 1, :], 0.0)
         ident = keep.tile([P, P], F32, name="ident")
         make_identity(nc, ident[:])
         nc.gpsimd.memset(nb_all[0 : P - 1, T // 2 : T], 0.0)
@@ -92,29 +96,26 @@ def tile_attend_mlpb_swiglu_topk_kernel(tc, qT, k_words, k_scales, c_words, c_sc
             nc.sync.dma_start(tile[:], q_view[:, :, halves[g]])
             return tile
 
-        nc.sync.dma_start(nb_all[P - 1 : P, :], nb[0:1, :])
+        load_scales(k_sc_all, k_scales)
+        load_scales(c_sc_all, c_scales)
         q_raw = [load_queries(0)]
-        load_scales(nc.sync, k_sc_all, k_scales, 0)
-        nc.scalar.activation(warm[:, 1:2], warm[:, 0:1], ACT.Silu)
-        k_all = load_words("k_all", k_words)
-        load_scales(nc.sync, c_sc_all, c_scales, C_ROW)
+        nc.sync.dma_start(us_row[P - 1 : P, :], us[0].rearrange("i o -> o i"))
+        nc.sync.dma_start(nb_all[P - 1 : P, :], nb[0:1, :])
+        k_all = load_words("k_all", k_words, "slot_v3")
         q_raw.append(load_queries(1))
-        nc.sync.dma_start(
-            us_rows[P - PACK : P, :].rearrange("t (m b) -> t m b", b=RUN),
-            us[0].rearrange("(m t b) o -> t m (b o)", t=PACK, b=RUN),
-        )
         c_all = load_words("c_all", c_words)
-        v_all = [load_values(j) for j in range(DV // P)]
+        nc.scalar.activation(warm[:, 1:2], warm[:, 0:1], ACT.Silu)
 
-        def gather_scales(window, name):
-            listed = sbuf(name + "_listed", [P, N], U8)
+        planes = sbuf("planes", [P, 2, PACK, P], U8)
+        plane_words = planes[:].rearrange("p s t m -> p (s t m)").bitcast(I32)
+
+        def gather_scales(window, name, side, slot):
+            listed = sbuf(name + "_listed", [P, N], U8, slot)
             nc.vector.tensor_copy(listed[:], window[:].indirect(offsets[:]))
-            plane = sbuf(name + "_plane", [P, PACK, P], U8)
             nc.vector.tensor_copy(
-                plane[:].rearrange("p t m -> p (t m)").bitcast(I32).rearrange("p (t m) -> p t m", t=PACK),
+                plane_words[:, side * P : (side + 1) * P].rearrange("p (t m) -> p t m", t=PACK),
                 listed[:].bitcast(I32).rearrange("p (m t) -> p t m", t=PACK),
             )
-            return plane
 
         def gather_words(window, name, dtype):
             words = sbuf(name, [P, PACK, P], dtype)
@@ -123,60 +124,84 @@ def tile_attend_mlpb_swiglu_topk_kernel(tc, qT, k_words, k_scales, c_words, c_sc
             )
             return words
 
+        gather_scales(k_sc_all, "k", 0, None)
+        gather_scales(c_sc_all, "c", 1, "slot_v0")
         nb_listed = gather_words(nb_all, "nb_listed", F32)
-        k_plane = gather_scales(k_sc_all, "k")
+        for r in range(4):
+            nc.sync.dma_start(plane_words[r:P:32, :], plane_words[P - ROWS + r : P : 4, :])
 
+
+        q_bf = [sbuf("q_bf0", [P, HALF, PACK], BF16, "slot_v1"), sbuf("q_bf1", [P, HALF, PACK], BF16)]
+        q_plane = sbuf("q_plane", [P, NQ], U8)
+        interleave(q_bf[0][:], q_raw[0][:])
+        us_dealt = sbuf("us_dealt", [P, PACK, P], F32)
+        nc.scalar.copy(
+            us_dealt[:].rearrange("p t (m b) -> p t m b", b=RUN), us_row[:].rearrange("p (m t b) -> p t m b", t=PACK, b=RUN)
+        )
+        us_ps = bank(5, [P, PACK, P], "us_ps")
+        for t in range(PACK):
+            nc.tensor.transpose(us_ps[:, t, :], us_dealt[:, t, :], ident[:])
+        us_col = sbuf("us_col", [P, PACK, 1], F32)
+        nc.scalar.copy(us_col[:], us_ps[:, :, P - 1 : P])
         nb_ps = bank(4, [P, PACK, P], "nb_ps")
         for t in range(PACK):
             nc.tensor.transpose(nb_ps[:, t, :], nb_listed[:, t, :], ident[:])
-        us_ps = bank(5, [P, P], "us_ps")
-        nc.tensor.transpose(us_ps[:], us_rows[:], ident[:])
-
-        q_bf = sbuf("q_bf", [P, NQ, PACK], BF16)
-        q_plane = sbuf("q_plane", [P, NQ], U8)
-        for g, cols in enumerate(halves):
-            interleave(q_bf[:, cols, :], q_raw[g][:])
-        nb_col = sbuf("nb_col", [P, PACK, 1], F32, "slot_q0")
-        nc.scalar.copy(nb_col[:], nb_ps[:, :, P - 1 : P])
-        us_col = sbuf("us_col", [P, PACK], F32)
-        nc.scalar.copy(us_col[:], us_ps[:, P - PACK : P])
 
         q_codes = [sbuf("q_codes0", [P, HALF], U32, "slot_s0")]
-        quantize(q_codes[0][:], q_plane[:, halves[0]], q_bf[:, halves[0], :])
+        quantize(q_codes[0][:], q_plane[:, halves[0]], q_bf[0][:])
         k_codes = gather_words(k_all, "k_codes", U32)
-        c_plane = gather_scales(c_sc_all, "c")
+        v_all = [load_values(j) for j in range(DV // P)]
+        interleave(q_bf[1][:], q_raw[1][:])
+        nb_col = sbuf("nb_col", [P, PACK, 1], F32, "slot_q1")
+        nc.scalar.copy(nb_col[:], nb_ps[:, :, P - 1 : P])
         q_codes.append(sbuf("q_codes1", [P, HALF], U32))
-        quantize(q_codes[1][:], q_plane[:, halves[1]], q_bf[:, halves[1], :])
-
-
-        def scores(codes, plane, t, index, name):
-            acc = bank(index, [P, 2, HALF], name)
-            for g, cols in enumerate(halves):
-                matmul(acc[:, g, :], codes[:, t, :], plane, q_codes[g][:], q_plane[:, cols])
-            return acc[:].rearrange("p g q -> p (g q)")
-
-        gate = sbuf("gate", [P, PACK, NQ], F32)
-        for t in range(PACK):
-            a_ps = scores(k_codes, k_plane[:, t, :], t, t, "a_ps")
-            nc.scalar.activation(gate[:, t, :], a_ps, ACT.Silu, bias=nb_col[:, t, :])
-
+        quantize(q_codes[1][:], q_plane[:, halves[1]], q_bf[1][:])
         c_codes = gather_words(c_all, "c_codes", U32)
 
-        y_rows = sbuf("y_rows", [P, PACK, NQ], BF16)
-        y_bf = sbuf("y_bf", [P, NQ, PACK], BF16)
-        y_codes = sbuf("y_codes", [P, NQ], U32)
+        def scores(codes, side, g, u, name):
+            acc = bank(PACK * side + 2 * g + u, [P, 2, HALF], name)
+            for h in range(2):
+                t = 2 * u + h
+                matmul(acc[:, h, :], codes[:, t, :], planes[:, side, t, :], q_codes[g][:], q_plane[:, halves[g]])
+            return acc
+
+        gate = {}
+        y_bf = [sbuf("y_bf0", [P, HALF, PACK], BF16)]
         y_plane = sbuf("y_plane", [P, NQ], U8)
-        for t in range(PACK):
-            z_ps = scores(c_codes, c_plane[C_ROW:P, t, :], t, PACK + t, "z_ps")
-            nc.vector.scalar_tensor_tensor(y_rows[:, t, :], z_ps, us_col[:, t : t + 1], gate[:, t, :], ALU.mult, ALU.mult)
-        for cols in halves:
-            interleave(y_bf[:, cols, :], y_rows[:, :, cols])
+
+        def gates(g):
+            for u in range(2):
+                a_ps = scores(k_codes, 0, g, u, "a_ps")
+                for h in range(2):
+                    t = 2 * u + h
+                    gate[g, t] = sbuf("gate%d%d" % (g, t), [P, HALF], F32, "slot_gate%d%d" % (g, t))
+                    nc.scalar.activation(gate[g, t][:], a_ps[:, h, :], ACT.Silu, bias=nb_col[:, t, :])
+
+        y_rows = [sbuf("y_rows%d" % g, [P, PACK, HALF], BF16) for g in range(2)]
+
+        gates(0)
+        for u in range(2):
+            z_ps = scores(c_codes, 1, 0, u, "z_ps")
+            for h in range(2):
+                t = 2 * u + h
+                nc.vector.scalar_tensor_tensor(
+                    y_rows[0][:, t, :], z_ps[:, h, :], us_col[:, t, :], gate[0, t][:], ALU.mult, ALU.mult
+                )
+        interleave_on_gpsimd(y_bf[0][:], y_rows[0][:])
+        gates(1)
+        for u in range(2):
+            z_ps = scores(c_codes, 1, 1, u, "z_ps")
+            for h in range(2):
+                t = 2 * u + h
+                scaled = sbuf("scaled%d" % t, [P, HALF], F32)
+                nc.scalar.activation(scaled[:], z_ps[:, h, :], ACT.Copy, scale=us_col[:, t, :])
+                nc.gpsimd.tensor_tensor(y_rows[1][:, t, :], scaled[:], gate[1, t][:], ALU.mult)
 
         v_bf = sbuf("v_bf", [P, DV, PACK], BF16)
         v_plane = sbuf("v_plane", [P, DV], U8)
 
-        def gather_values(j):
-            listed = sbuf("v_listed%d" % j, [P, 2, P, 2], BF16)
+        def gather_values(j, slot=None):
+            listed = sbuf("v_listed%d" % j, [P, 2, P, 2], BF16, slot)
             nc.vector.tensor_copy(listed[:].rearrange("e u (m b) h -> e m u h b", b=RUN), v_all[j][:].indirect(offsets[:]))
             words = listed[:].rearrange("e u m h -> e (u m h)").bitcast(F32)
             turned = bank(j, [P, 2, P], "v_turned")
@@ -185,11 +210,6 @@ def tile_attend_mlpb_swiglu_topk_kernel(tc, qT, k_words, k_scales, c_words, c_sc
             dst = v_bf[:, blocks[j], :].rearrange("p e t -> p (e t)").bitcast(F32)
             nc.scalar.copy(dst.rearrange("p (e u) -> p e u", u=2), turned[:].rearrange("p u e -> p e u"))
 
-        def quantize_values(cols, slot):
-            codes = sbuf("v_codes%d" % cols.start, [P, cols.stop - cols.start], U32, slot)
-            quantize(codes[:], v_plane[:, cols], v_bf[:, cols, :])
-            return codes
-
         out_view = out[0].rearrange("(b p) e -> p b e", p=P)
 
         def multiply(cols, codes, rows, index, engine_copy):
@@ -197,24 +217,31 @@ def tile_attend_mlpb_swiglu_topk_kernel(tc, qT, k_words, k_scales, c_words, c_sc
             count = rows.stop - rows.start
             o_ps = bank(index, [P, count, width], "o_ps")
             for b in range(count):
-                block = blocks[rows.start + b]
-                matmul(o_ps[:, b, :], y_codes[:, block], y_plane[:, block], codes[:], v_plane[:, cols])
+                g, within = divmod(rows.start + b, 2)
+                matmul(o_ps[:, b, :], y_codes[g][:, blocks[within]], y_plane[:, blocks[rows.start + b]], codes, v_plane[:, cols])
             res = sbuf("res%d_%d" % (cols.start, rows.start), [P, count, width], F32)
             engine_copy(res[:], o_ps[:])
             nc.sync.dma_start(out_view[:, rows, cols], res[:])
 
-        gather_values(0)
-        quantize(y_codes[:, halves[0]], y_plane[:, halves[0]], y_bf[:, halves[0], :])
-        gather_values(1)
-        quantize(y_codes[:, halves[1]], y_plane[:, halves[1]], y_bf[:, halves[1], :])
+        gather_values(0, "slot_gate02")
+        gather_values(1, "slot_l1")
+        y_bf.append(sbuf("y_bf1", [P, HALF, PACK], BF16, "slot_l1"))
+        interleave(y_bf[1][:], y_rows[1][:])
+        y_first = sbuf("y_first", [P, HALF], U32, "slot_v1")
+        quantize(y_first[:], y_plane[:, halves[0]], y_bf[0][:])
         gather_values(2)
         first = slice(0, 2 * P)
-        codes = quantize_values(first, "slot_v2")
+        codes01 = sbuf("v_codes01", [P, 2 * P], U32, "slot_v2")
+        quantize(codes01[:], v_plane[:, first], v_bf[:, first, :])
+        late = sbuf("late", [P, HALF + P], U32, "slot_v3")
+        y_codes = [y_first[:], late[:, 0:HALF]]
+        multiply(first, codes01[:], slice(0, 2), 4, nc.scalar.copy)
         gather_values(3)
-        multiply(first, codes, slice(0, 2), 4, nc.scalar.copy)
-        multiply(first, codes, slice(2, 4), 5, nc.scalar.copy)
-        codes2 = quantize_values(blocks[2], "slot_v3")
-        codes3 = quantize_values(blocks[3], None)
-        multiply(blocks[2], codes2, slice(0, 4), 6, nc.vector.tensor_copy)
-        multiply(blocks[3], codes3, slice(0, 2), 7, nc.scalar.copy)
-        multiply(blocks[3], codes3, slice(2, 4), 0, nc.vector.tensor_copy)
+        codes3 = sbuf("v_codes3", [P, P], U32)
+        quantize(late[:, 0:HALF], y_plane[:, halves[1]], y_bf[1][:])
+        quantize(late[:, HALF : HALF + P], v_plane[:, blocks[2]], v_bf[:, blocks[2], :])
+        quantize(codes3[:], v_plane[:, blocks[3]], v_bf[:, blocks[3], :])
+        multiply(first, codes01[:], slice(2, 4), 5, nc.scalar.copy)
+        multiply(blocks[2], late[:, HALF : HALF + P], slice(0, 4), 6, nc.vector.tensor_copy)
+        multiply(blocks[3], codes3[:], slice(0, 2), 7, nc.scalar.copy)
+        multiply(blocks[3], codes3[:], slice(2, 4), 0, nc.vector.tensor_copy)

@@ -64,11 +64,6 @@ def tile_attend_mlpb_swiglu_topk_kernel(tc, qT, k_words, k_scales, c_words, c_sc
         def interleave(dst, src):
             nc.scalar.copy(dst.rearrange("p (c i) t -> p c t i", i=RUN), src.rearrange("p t (c i) -> p c t i", i=RUN))
 
-        def interleave_on_gpsimd(dst, src):
-            nc.gpsimd.tensor_scalar(
-                out=dst, in0=src.rearrange("p t c -> p c t"), scalar1=1.0, scalar2=0.0, op0=ALU.mult, op1=ALU.add
-            )
-
         halves = [slice(h * HALF, (h + 1) * HALF) for h in range(2)]
         blocks = [slice(j * P, (j + 1) * P) for j in range(DV // P)]
 
@@ -76,41 +71,35 @@ def tile_attend_mlpb_swiglu_topk_kernel(tc, qT, k_words, k_scales, c_words, c_sc
         nc.sync.dma_start(offsets[:], offs)
 
         k_sc_all = sbuf("k_sc_all", [P, T], U8)
-        c_sc_all = sbuf("c_sc_all", [P, T], U8, "slot_s0")
-        nb_all = sbuf("nb_all", [P, T], F32, "slot_v2")
-        us_row = sbuf("us_row", [P, N], F32)
+        c_sc_all = sbuf("c_sc_all", [P, T], U8)
+        nb_all = sbuf("nb_all", [P, T], F32, "slot_nb")
+        us_row = sbuf("us_row", [1, N], F32)
         warm = keep.tile([P, 2], F32, name="warm")
         nc.vector.memset(k_sc_all[0 : P - ROWS, :].bitcast(I32), 0)
         nc.vector.memset(c_sc_all[0 : P - ROWS, :].bitcast(I32), 0)
         nc.vector.memset(warm[:, 0:1], 0.0)
         nc.vector.memset(nb_all[0 : P - 1, 0 : T // 2], 0.0)
-        nc.gpsimd.memset(us_row[0 : P - 1, :], 0.0)
+        nc.gpsimd.memset(nb_all[0 : P - 1, T // 2 : T], 0.0)
         ident = keep.tile([P, P], F32, name="ident")
         make_identity(nc, ident[:])
-        nc.gpsimd.memset(nb_all[0 : P - 1, T // 2 : T], 0.0)
-
-        q_view = qT[0].rearrange("(p j) q -> p j q", j=PACK)
-
-        def load_queries(g):
-            tile = sbuf("q_raw%d" % g, [P, PACK, HALF], F32, "slot_q%d" % g)
-            nc.sync.dma_start(tile[:], q_view[:, :, halves[g]])
-            return tile
 
         load_scales(k_sc_all, k_scales)
         load_scales(c_sc_all, c_scales)
-        q_raw = [load_queries(0)]
-        nc.sync.dma_start(us_row[P - 1 : P, :], us[0].rearrange("i o -> o i"))
+        q_raw = sbuf("q_raw", [P, PACK, NQ], F32, "slot_q")
+        nc.sync.dma_start(q_raw[:], qT[0].rearrange("(p j) q -> p j q", j=PACK))
         nc.sync.dma_start(nb_all[P - 1 : P, :], nb[0:1, :])
-        k_all = load_words("k_all", k_words, "slot_v3")
-        q_raw.append(load_queries(1))
+        nc.sync.dma_start(us_row[:], us[0].rearrange("i o -> o i"))
+        k_all = load_words("k_all", k_words, "slot_k")
         c_all = load_words("c_all", c_words)
         nc.scalar.activation(warm[:, 1:2], warm[:, 0:1], ACT.Silu)
 
         planes = sbuf("planes", [P, 2, PACK, P], U8)
         plane_words = planes[:].rearrange("p s t m -> p (s t m)").bitcast(I32)
+        k_plane = planes[:, 0]
+        c_plane = planes[:, 1]
 
-        def gather_scales(window, name, side, slot):
-            listed = sbuf(name + "_listed", [P, N], U8, slot)
+        def gather_scales(window, name, side):
+            listed = sbuf(name + "_listed", [P, N], U8)
             nc.vector.tensor_copy(listed[:], window[:].indirect(offsets[:]))
             nc.vector.tensor_copy(
                 plane_words[:, side * P : (side + 1) * P].rearrange("p (t m) -> p t m", t=PACK),
@@ -124,84 +113,71 @@ def tile_attend_mlpb_swiglu_topk_kernel(tc, qT, k_words, k_scales, c_words, c_sc
             )
             return words
 
-        gather_scales(k_sc_all, "k", 0, None)
-        gather_scales(c_sc_all, "c", 1, "slot_v0")
-        nb_listed = gather_words(nb_all, "nb_listed", F32)
+        gather_scales(k_sc_all, "k", 0)
+        gather_scales(c_sc_all, "c", 1)
         for r in range(4):
             nc.sync.dma_start(plane_words[r:P:32, :], plane_words[P - ROWS + r : P : 4, :])
+        rows = gather_words(nb_all, "rows", F32)
+        v_all = [load_values(j) for j in range(DV // P)]
 
-
-        q_bf = [sbuf("q_bf0", [P, HALF, PACK], BF16, "slot_v1"), sbuf("q_bf1", [P, HALF, PACK], BF16)]
+        q_bf = [sbuf("q_bf%d" % g, [P, HALF, PACK], BF16) for g in range(2)]
         q_plane = sbuf("q_plane", [P, NQ], U8)
-        interleave(q_bf[0][:], q_raw[0][:])
-        us_dealt = sbuf("us_dealt", [P, PACK, P], F32)
-        nc.scalar.copy(
-            us_dealt[:].rearrange("p t (m b) -> p t m b", b=RUN), us_row[:].rearrange("p (m t b) -> p t m b", t=PACK, b=RUN)
+        for g in range(2):
+            interleave(q_bf[g][:], q_raw[:, :, halves[g]])
+        nc.gpsimd.tensor_scalar(
+            out=rows[0:1].rearrange("p t (m b) -> p t m b", b=RUN),
+            in0=us_row[:].rearrange("p (m t b) -> p t m b", t=PACK, b=RUN),
+            scalar1=1.0, scalar2=0.0, op0=ALU.mult, op1=ALU.add,
         )
-        us_ps = bank(5, [P, PACK, P], "us_ps")
+        rows_ps = bank(4, [P, PACK, P], "rows_ps")
         for t in range(PACK):
-            nc.tensor.transpose(us_ps[:, t, :], us_dealt[:, t, :], ident[:])
-        us_col = sbuf("us_col", [P, PACK, 1], F32)
-        nc.scalar.copy(us_col[:], us_ps[:, :, P - 1 : P])
-        nb_ps = bank(4, [P, PACK, P], "nb_ps")
-        for t in range(PACK):
-            nc.tensor.transpose(nb_ps[:, t, :], nb_listed[:, t, :], ident[:])
+            nc.tensor.transpose(rows_ps[:, t, :], rows[:, t, :], ident[:])
+        cols = sbuf("cols", [P, PACK, 2], F32, "slot_q")
+        nc.scalar.copy(cols[:], rows_ps[:, :, 0 : P : P - 1])
 
-        q_codes = [sbuf("q_codes0", [P, HALF], U32, "slot_s0")]
+        q_codes = [sbuf("q_codes0", [P, HALF], U32, "slot_nb")]
         quantize(q_codes[0][:], q_plane[:, halves[0]], q_bf[0][:])
         k_codes = gather_words(k_all, "k_codes", U32)
-        v_all = [load_values(j) for j in range(DV // P)]
-        interleave(q_bf[1][:], q_raw[1][:])
-        nb_col = sbuf("nb_col", [P, PACK, 1], F32, "slot_q1")
-        nc.scalar.copy(nb_col[:], nb_ps[:, :, P - 1 : P])
-        q_codes.append(sbuf("q_codes1", [P, HALF], U32))
+        q_codes.append(sbuf("q_codes1", [P, HALF], U32, "slot_k"))
         quantize(q_codes[1][:], q_plane[:, halves[1]], q_bf[1][:])
         c_codes = gather_words(c_all, "c_codes", U32)
 
-        def scores(codes, side, g, u, name):
-            acc = bank(PACK * side + 2 * g + u, [P, 2, HALF], name)
+        def scores(codes, plane, g, u, index, name):
+            acc = bank(index, [P, 2, HALF], name)
             for h in range(2):
-                t = 2 * u + h
-                matmul(acc[:, h, :], codes[:, t, :], planes[:, side, t, :], q_codes[g][:], q_plane[:, halves[g]])
+                matmul(acc[:, h, :], codes[:, 2 * u + h, :], plane[:, 2 * u + h, :], q_codes[g][:], q_plane[:, halves[g]])
             return acc
 
-        gate = {}
-        y_bf = [sbuf("y_bf0", [P, HALF, PACK], BF16)]
-        y_plane = sbuf("y_plane", [P, NQ], U8)
+        def gate(g, t, scores_t):
+            tile = sbuf("gate%d%d" % (g, t), [P, HALF], F32)
+            nc.scalar.activation(tile[:], scores_t, ACT.Silu, bias=cols[:, t, 1:2])
+            return tile
 
-        def gates(g):
-            for u in range(2):
-                a_ps = scores(k_codes, 0, g, u, "a_ps")
-                for h in range(2):
-                    t = 2 * u + h
-                    gate[g, t] = sbuf("gate%d%d" % (g, t), [P, HALF], F32, "slot_gate%d%d" % (g, t))
-                    nc.scalar.activation(gate[g, t][:], a_ps[:, h, :], ACT.Silu, bias=nb_col[:, t, :])
-
-        y_rows = [sbuf("y_rows%d" % g, [P, PACK, HALF], BF16) for g in range(2)]
-
-        gates(0)
+        scaled = sbuf("scaled", [P, PACK, HALF], F32)
         for u in range(2):
-            z_ps = scores(c_codes, 1, 0, u, "z_ps")
+            a_ps = scores(k_codes, k_plane, 0, u, u, "a_ps")
             for h in range(2):
                 t = 2 * u + h
-                nc.vector.scalar_tensor_tensor(
-                    y_rows[0][:, t, :], z_ps[:, h, :], us_col[:, t, :], gate[0, t][:], ALU.mult, ALU.mult
+                nc.gpsimd.tensor_scalar(
+                    out=scaled[:, t, :], in0=gate(0, t, a_ps[:, h, :])[:], scalar1=cols[:, t, 0:1], scalar2=0.0,
+                    op0=ALU.mult, op1=ALU.add,
                 )
-        interleave_on_gpsimd(y_bf[0][:], y_rows[0][:])
-        gates(1)
+        y_rows = sbuf("y_rows", [P, PACK, HALF], BF16)
         for u in range(2):
-            z_ps = scores(c_codes, 1, 1, u, "z_ps")
+            a_ps = scores(k_codes, k_plane, 1, u, 2 + u, "a_ps")
+            z_ps = scores(c_codes, c_plane, 1, u, PACK + 2 + u, "z_ps")
             for h in range(2):
                 t = 2 * u + h
-                scaled = sbuf("scaled%d" % t, [P, HALF], F32)
-                nc.scalar.activation(scaled[:], z_ps[:, h, :], ACT.Copy, scale=us_col[:, t, :])
-                nc.gpsimd.tensor_tensor(y_rows[1][:, t, :], scaled[:], gate[1, t][:], ALU.mult)
+                gated = gate(1, t, a_ps[:, h, :])
+                layer = sbuf("layer%d" % t, [P, HALF], F32)
+                nc.scalar.activation(layer[:], z_ps[:, h, :], ACT.Copy, scale=cols[:, t, 0:1])
+                nc.gpsimd.tensor_tensor(y_rows[:, t, :], layer[:], gated[:], ALU.mult)
 
         v_bf = sbuf("v_bf", [P, DV, PACK], BF16)
         v_plane = sbuf("v_plane", [P, DV], U8)
 
-        def gather_values(j, slot=None):
-            listed = sbuf("v_listed%d" % j, [P, 2, P, 2], BF16, slot)
+        def gather_values(j):
+            listed = sbuf("v_listed%d" % j, [P, 2, P, 2], BF16, "slot_l%d" % j)
             nc.vector.tensor_copy(listed[:].rearrange("e u (m b) h -> e m u h b", b=RUN), v_all[j][:].indirect(offsets[:]))
             words = listed[:].rearrange("e u m h -> e (u m h)").bitcast(F32)
             turned = bank(j, [P, 2, P], "v_turned")
@@ -209,6 +185,23 @@ def tile_attend_mlpb_swiglu_topk_kernel(tc, qT, k_words, k_scales, c_words, c_sc
                 nc.tensor.transpose(turned[:, u, :], words[:, u * P : (u + 1) * P], ident[:])
             dst = v_bf[:, blocks[j], :].rearrange("p e t -> p (e t)").bitcast(F32)
             nc.scalar.copy(dst.rearrange("p (e u) -> p e u", u=2), turned[:].rearrange("p u e -> p e u"))
+
+        gather_values(0)
+        y_bf = [sbuf("y_bf0", [P, HALF, PACK], BF16, "slot_v0")]
+        for b in range(2):
+            z_ps = bank(PACK + b, [P, PACK, P], "z_ps")
+            for t in range(PACK):
+                matmul(z_ps[:, t, :], c_codes[:, t, :], c_plane[:, t, :], q_codes[0][:, blocks[b]], q_plane[:, blocks[b]])
+            nc.vector.tensor_tensor(
+                y_bf[0][:, blocks[b], :].rearrange("p (c i) t -> p c t i", i=2),
+                z_ps[:].rearrange("p t (c i) -> p c t i", i=2),
+                scaled[:, :, blocks[b]].rearrange("p t (c i) -> p c t i", i=2),
+                ALU.mult,
+            )
+        y_bf.append(sbuf("y_bf1", [P, HALF, PACK], BF16, "slot_l0"))
+        interleave(y_bf[1][:], y_rows[:])
+        gather_values(1)
+        y_plane = sbuf("y_plane", [P, NQ], U8)
 
         out_view = out[0].rearrange("(b p) e -> p b e", p=P)
 
@@ -223,25 +216,22 @@ def tile_attend_mlpb_swiglu_topk_kernel(tc, qT, k_words, k_scales, c_words, c_sc
             engine_copy(res[:], o_ps[:])
             nc.sync.dma_start(out_view[:, rows, cols], res[:])
 
-        gather_values(0, "slot_gate02")
-        gather_values(1, "slot_l1")
-        y_bf.append(sbuf("y_bf1", [P, HALF, PACK], BF16, "slot_l1"))
-        interleave(y_bf[1][:], y_rows[1][:])
         y_first = sbuf("y_first", [P, HALF], U32, "slot_v1")
         quantize(y_first[:], y_plane[:, halves[0]], y_bf[0][:])
         gather_values(2)
         first = slice(0, 2 * P)
-        codes01 = sbuf("v_codes01", [P, 2 * P], U32, "slot_v2")
-        quantize(codes01[:], v_plane[:, first], v_bf[:, first, :])
-        late = sbuf("late", [P, HALF + P], U32, "slot_v3")
+        late = sbuf("late", [P, 2 * HALF], U32, "slot_v2")
         y_codes = [y_first[:], late[:, 0:HALF]]
-        multiply(first, codes01[:], slice(0, 2), 4, nc.scalar.copy)
+        codes01 = late[:, HALF : 2 * HALF]
+        quantize(y_codes[1], y_plane[:, halves[1]], y_bf[1][:])
+        quantize(codes01, v_plane[:, first], v_bf[:, first, :])
+        multiply(first, codes01, slice(0, 2), 4, nc.scalar.copy)
+        multiply(first, codes01, slice(2, 4), 5, nc.scalar.copy)
         gather_values(3)
+        codes2 = sbuf("v_codes2", [P, P], U32, "slot_v3")
+        quantize(codes2[:], v_plane[:, blocks[2]], v_bf[:, blocks[2], :])
+        multiply(blocks[2], codes2[:], slice(0, 4), 6, nc.scalar.copy)
         codes3 = sbuf("v_codes3", [P, P], U32)
-        quantize(late[:, 0:HALF], y_plane[:, halves[1]], y_bf[1][:])
-        quantize(late[:, HALF : HALF + P], v_plane[:, blocks[2]], v_bf[:, blocks[2], :])
         quantize(codes3[:], v_plane[:, blocks[3]], v_bf[:, blocks[3], :])
-        multiply(first, codes01[:], slice(2, 4), 5, nc.scalar.copy)
-        multiply(blocks[2], late[:, HALF : HALF + P], slice(0, 4), 6, nc.vector.tensor_copy)
-        multiply(blocks[3], codes3[:], slice(0, 2), 7, nc.scalar.copy)
-        multiply(blocks[3], codes3[:], slice(2, 4), 0, nc.vector.tensor_copy)
+        multiply(blocks[3], codes3[:], slice(0, 2), 7, nc.vector.tensor_copy)
+        multiply(blocks[3], codes3[:], slice(2, 4), 0, nc.scalar.copy)

@@ -158,80 +158,94 @@ def tile_attend_mlpb_swiglu_topk_kernel(tc, qT, k_words, k_scales, c_words, c_sc
             a_ps = scores(k_codes, k_plane, 0, u, u, "a_ps")
             for h in range(2):
                 t = 2 * u + h
+                gated = gate(0, t, a_ps[:, h, :])
                 nc.gpsimd.tensor_scalar(
-                    out=scaled[:, t, :], in0=gate(0, t, a_ps[:, h, :])[:], scalar1=cols[:, t, 0:1], scalar2=0.0,
-                    op0=ALU.mult, op1=ALU.add,
+                    out=scaled[:, t, :], in0=gated[:], scalar1=cols[:, t, 0:1], scalar2=0.0, op0=ALU.mult, op1=ALU.add
                 )
+        staged = sbuf("staged", [P, 3 * P, PACK], BF16)
+        v_last = sbuf("v_last", [P, P, PACK], BF16, "slot_last")
+        v_bf = [staged[:, blocks[j], :] for j in range(3)] + [v_last[:]]
         y_rows = sbuf("y_rows", [P, PACK, HALF], BF16)
-        for u in range(2):
+
+        def second_half(u, slot):
             a_ps = scores(k_codes, k_plane, 1, u, 2 + u, "a_ps")
             z_ps = scores(c_codes, c_plane, 1, u, PACK + 2 + u, "z_ps")
+            gated = sbuf("gated%d" % u, [P, 2, HALF], F32)
+            layer = sbuf("layer%d" % u, [P, 2, HALF], F32, slot)
             for h in range(2):
                 t = 2 * u + h
-                gated = gate(1, t, a_ps[:, h, :])
-                layer = sbuf("layer%d" % t, [P, HALF], F32)
-                nc.scalar.activation(layer[:], z_ps[:, h, :], ACT.Copy, scale=cols[:, t, 0:1])
-                nc.gpsimd.tensor_tensor(y_rows[:, t, :], layer[:], gated[:], ALU.mult)
+                nc.scalar.activation(gated[:, h, :], a_ps[:, h, :], ACT.Silu, bias=cols[:, t, 1:2])
+                nc.scalar.activation(layer[:, h, :], z_ps[:, h, :], ACT.Copy, scale=cols[:, t, 0:1])
+            nc.gpsimd.tensor_tensor(y_rows[:, 2 * u : 2 * u + 2, :], layer[:], gated[:], ALU.mult)
 
-        v_bf = sbuf("v_bf", [P, DV, PACK], BF16)
-        v_plane = sbuf("v_plane", [P, DV], U8)
+        yv_plane = sbuf("yv_plane", [P, NQ + DV], U8)
+        y_plane = yv_plane[:, 0:NQ]
+        v_plane = yv_plane[:, NQ : NQ + DV]
 
-        def gather_values(j):
+        def turn_values(j):
             listed = sbuf("v_listed%d" % j, [P, 2, P, 2], BF16, "slot_l%d" % j)
             nc.vector.tensor_copy(listed[:].rearrange("e u (m b) h -> e m u h b", b=RUN), v_all[j][:].indirect(offsets[:]))
             words = listed[:].rearrange("e u m h -> e (u m h)").bitcast(F32)
             turned = bank(j, [P, 2, P], "v_turned")
             for u in range(2):
                 nc.tensor.transpose(turned[:, u, :], words[:, u * P : (u + 1) * P], ident[:])
-            dst = v_bf[:, blocks[j], :].rearrange("p e t -> p (e t)").bitcast(F32)
+            return turned
+
+        def stage_values(j, turned):
+            dst = v_bf[j].rearrange("p e t -> p (e t)").bitcast(F32)
             nc.scalar.copy(dst.rearrange("p (e u) -> p e u", u=2), turned[:].rearrange("p u e -> p e u"))
 
-        gather_values(0)
-        y_bf = [sbuf("y_bf0", [P, HALF, PACK], BF16, "slot_v0")]
+        def gather_values(j):
+            stage_values(j, turn_values(j))
+
+        second_half(0, None)
+        turned0 = turn_values(0)
+        second_half(1, "slot_l0")
+        stage_values(0, turned0)
+        y_bf = sbuf("y_bf", [P, NQ, PACK], BF16, "slot_v0")
         for b in range(2):
             z_ps = bank(PACK + b, [P, PACK, P], "z_ps")
             for t in range(PACK):
                 matmul(z_ps[:, t, :], c_codes[:, t, :], c_plane[:, t, :], q_codes[0][:, blocks[b]], q_plane[:, blocks[b]])
             nc.vector.tensor_tensor(
-                y_bf[0][:, blocks[b], :].rearrange("p (c i) t -> p c t i", i=2),
+                y_bf[:, blocks[b], :].rearrange("p (c i) t -> p c t i", i=2),
                 z_ps[:].rearrange("p t (c i) -> p c t i", i=2),
                 scaled[:, :, blocks[b]].rearrange("p t (c i) -> p c t i", i=2),
                 ALU.mult,
             )
-        y_bf.append(sbuf("y_bf1", [P, HALF, PACK], BF16, "slot_l0"))
-        interleave(y_bf[1][:], y_rows[:])
+        interleave(y_bf[:, halves[1], :], y_rows[:])
         gather_values(1)
-        y_plane = sbuf("y_plane", [P, NQ], U8)
 
         out_view = out[0].rearrange("(b p) e -> p b e", p=P)
 
-        def multiply(cols, codes, rows, index, engine_copy):
+        def multiply(cols, codes, rows, index, engine_copy, res=None):
             width = cols.stop - cols.start
             count = rows.stop - rows.start
             o_ps = bank(index, [P, count, width], "o_ps")
             for b in range(count):
                 g, within = divmod(rows.start + b, 2)
                 matmul(o_ps[:, b, :], y_codes[g][:, blocks[within]], y_plane[:, blocks[rows.start + b]], codes, v_plane[:, cols])
-            res = sbuf("res%d_%d" % (cols.start, rows.start), [P, count, width], F32)
-            engine_copy(res[:], o_ps[:])
-            nc.sync.dma_start(out_view[:, rows, cols], res[:])
+            if res is None:
+                res = sbuf("res%d_%d" % (cols.start, rows.start), [P, count, width], F32)[:]
+            engine_copy(res, o_ps[:])
+            nc.sync.dma_start(out_view[:, rows, cols], res)
 
-        y_first = sbuf("y_first", [P, HALF], U32, "slot_v1")
-        quantize(y_first[:], y_plane[:, halves[0]], y_bf[0][:])
         gather_values(2)
         first = slice(0, 2 * P)
-        late = sbuf("late", [P, 2 * HALF], U32, "slot_v2")
-        y_codes = [y_first[:], late[:, 0:HALF]]
-        codes01 = late[:, HALF : 2 * HALF]
-        quantize(y_codes[1], y_plane[:, halves[1]], y_bf[1][:])
-        quantize(codes01, v_plane[:, first], v_bf[:, first, :])
+        late = sbuf("late", [P, NQ + 2 * P], U32, "slot_v2")
+        y_codes = [late[:, halves[0]], late[:, halves[1]]]
+        codes01 = late[:, NQ : NQ + 2 * P]
+        quantize(late[:, 0:NQ], y_plane, y_bf[:])
+        quantize(codes01, v_plane[:, first], staged[:, first, :])
         multiply(first, codes01, slice(0, 2), 4, nc.scalar.copy)
         multiply(first, codes01, slice(2, 4), 5, nc.scalar.copy)
         gather_values(3)
         codes2 = sbuf("v_codes2", [P, P], U32, "slot_v3")
-        quantize(codes2[:], v_plane[:, blocks[2]], v_bf[:, blocks[2], :])
-        multiply(blocks[2], codes2[:], slice(0, 4), 6, nc.scalar.copy)
+        quantize(codes2[:], v_plane[:, blocks[2]], v_bf[2])
+        multiply(blocks[2], codes2[:], slice(0, 2), 6, nc.scalar.copy)
         codes3 = sbuf("v_codes3", [P, P], U32)
-        quantize(codes3[:], v_plane[:, blocks[3]], v_bf[:, blocks[3], :])
+        quantize(codes3[:], v_plane[:, blocks[3]], v_bf[3])
+        held = sbuf("held", [P, 2, P], F32, "slot_last")
+        multiply(blocks[2], codes2[:], slice(2, 4), 1, nc.vector.tensor_copy, held[:])
         multiply(blocks[3], codes3[:], slice(0, 2), 7, nc.vector.tensor_copy)
         multiply(blocks[3], codes3[:], slice(2, 4), 0, nc.scalar.copy)

@@ -23,6 +23,7 @@ D = 512
 DV = 512
 HALF = NQ // 2
 ROWS = 16
+AHEAD = 3 * T // 4
 FLOPS = 2 * N * NQ * (2 * D + DV)
 BYTES = 4 * D * NQ + 2 * (D * T + D * T // 32) + 4 * DV * T + 4 * T + 4 * N + 2 * N + 4 * NQ * DV
 
@@ -71,7 +72,7 @@ def tile_attend_mlpb_swiglu_topk_kernel(tc, qT, k_words, k_scales, c_words, c_sc
         nc.sync.dma_start(offsets[:], offs)
 
         k_sc_all = sbuf("k_sc_all", [P, T], U8)
-        c_sc_all = sbuf("c_sc_all", [P, T], U8)
+        c_sc_all = sbuf("c_sc_all", [P, T], U8, "slot_cs")
         nb_all = sbuf("nb_all", [P, T], F32, "slot_nb")
         us_row = sbuf("us_row", [1, N], F32)
         warm = keep.tile([P, 2], F32, name="warm")
@@ -90,20 +91,25 @@ def tile_attend_mlpb_swiglu_topk_kernel(tc, qT, k_words, k_scales, c_words, c_sc
         nc.sync.dma_start(nb_all[P - 1 : P, :], nb[0:1, :])
         nc.sync.dma_start(us_row[:], us[0].rearrange("i o -> o i"))
         k_all = load_words("k_all", k_words, "slot_k")
-        c_all = load_words("c_all", c_words)
+        c_all = sbuf("c_all", [P, T], I32)
+        c_view = c_words[0].rearrange("p t r -> p (t r)").bitcast(I32)
+        nc.sync.dma_start(c_all[:, 0:AHEAD], c_view[:, 0:AHEAD])
         nc.scalar.activation(warm[:, 1:2], warm[:, 0:1], ACT.Silu)
 
-        planes = sbuf("planes", [P, 2, PACK, P], U8)
+        def gather_scales(window, name):
+            listed = sbuf(name + "_listed", [P, N], U8)
+            nc.vector.tensor_copy(listed[:], window[:].indirect(offsets[:]))
+            return listed
+
+        listed_scales = [gather_scales(k_sc_all, "k"), gather_scales(c_sc_all, "c")]
+        planes = sbuf("planes", [P, 2, PACK, P], U8, "slot_cs")
         plane_words = planes[:].rearrange("p s t m -> p (s t m)").bitcast(I32)
         k_plane = planes[:, 0]
         c_plane = planes[:, 1]
-
-        def gather_scales(window, name, side):
-            listed = sbuf(name + "_listed", [P, N], U8)
-            nc.vector.tensor_copy(listed[:], window[:].indirect(offsets[:]))
+        for side in range(2):
             nc.vector.tensor_copy(
                 plane_words[:, side * P : (side + 1) * P].rearrange("p (t m) -> p t m", t=PACK),
-                listed[:].bitcast(I32).rearrange("p (m t) -> p t m", t=PACK),
+                listed_scales[side][:].bitcast(I32).rearrange("p (m t) -> p t m", t=PACK),
             )
 
         def gather_words(window, name, dtype):
@@ -113,10 +119,9 @@ def tile_attend_mlpb_swiglu_topk_kernel(tc, qT, k_words, k_scales, c_words, c_sc
             )
             return words
 
-        gather_scales(k_sc_all, "k", 0)
-        gather_scales(c_sc_all, "c", 1)
         for r in range(4):
             nc.sync.dma_start(plane_words[r:P:32, :], plane_words[P - ROWS + r : P : 4, :])
+        nc.sync.dma_start(c_all[:, AHEAD:T], c_view[:, AHEAD:T])
         rows = gather_words(nb_all, "rows", F32)
         v_all = [load_values(j) for j in range(DV // P)]
 
@@ -124,10 +129,8 @@ def tile_attend_mlpb_swiglu_topk_kernel(tc, qT, k_words, k_scales, c_words, c_sc
         q_plane = sbuf("q_plane", [P, NQ], U8)
         for g in range(2):
             interleave(q_bf[g][:], q_raw[:, :, halves[g]])
-        nc.gpsimd.tensor_scalar(
-            out=rows[0:1].rearrange("p t (m b) -> p t m b", b=RUN),
-            in0=us_row[:].rearrange("p (m t b) -> p t m b", t=PACK, b=RUN),
-            scalar1=1.0, scalar2=0.0, op0=ALU.mult, op1=ALU.add,
+        nc.scalar.copy(
+            rows[0:1].rearrange("p t (m b) -> p t m b", b=RUN), us_row[:].rearrange("p (m t b) -> p t m b", t=PACK, b=RUN)
         )
         rows_ps = bank(4, [P, PACK, P], "rows_ps")
         for t in range(PACK):
@@ -167,16 +170,18 @@ def tile_attend_mlpb_swiglu_topk_kernel(tc, qT, k_words, k_scales, c_words, c_sc
         v_bf = [staged[:, blocks[j], :] for j in range(3)] + [v_last[:]]
         y_rows = sbuf("y_rows", [P, PACK, HALF], BF16)
 
-        def second_half(u, slot):
+        gated = [sbuf("gated%d" % u, [P, 2, HALF], F32) for u in range(2)]
+        for u in range(2):
             a_ps = scores(k_codes, k_plane, 1, u, 2 + u, "a_ps")
+            for h in range(2):
+                nc.scalar.activation(gated[u][:, h, :], a_ps[:, h, :], ACT.Silu, bias=cols[:, 2 * u + h, 1:2])
+
+        def second_half(u, slot):
             z_ps = scores(c_codes, c_plane, 1, u, PACK + 2 + u, "z_ps")
-            gated = sbuf("gated%d" % u, [P, 2, HALF], F32)
             layer = sbuf("layer%d" % u, [P, 2, HALF], F32, slot)
             for h in range(2):
-                t = 2 * u + h
-                nc.scalar.activation(gated[:, h, :], a_ps[:, h, :], ACT.Silu, bias=cols[:, t, 1:2])
-                nc.scalar.activation(layer[:, h, :], z_ps[:, h, :], ACT.Copy, scale=cols[:, t, 0:1])
-            nc.gpsimd.tensor_tensor(y_rows[:, 2 * u : 2 * u + 2, :], layer[:], gated[:], ALU.mult)
+                nc.scalar.activation(layer[:, h, :], z_ps[:, h, :], ACT.Copy, scale=cols[:, 2 * u + h, 0:1])
+            nc.gpsimd.tensor_tensor(y_rows[:, 2 * u : 2 * u + 2, :], layer[:], gated[u][:], ALU.mult)
 
         yv_plane = sbuf("yv_plane", [P, NQ + DV], U8)
         y_plane = yv_plane[:, 0:NQ]

@@ -40,8 +40,8 @@ def tile_attend_mlpb_swiglu_topk_kernel(tc, qT, k_words, k_scales, c_words, c_sc
         def bank(index, shape, name):
             return psum.tile(shape, F32, name=name, tag="bank%d" % index)
 
-        def load_scales(tile, scales):
-            nc.sync.dma_start(tile[P - ROWS : P, :].bitcast(I32), scales[0].bitcast(I32))
+        def load_scales(tile, scales, queue):
+            queue.dma_start(tile[P - ROWS : P, :].bitcast(I32), scales[0].bitcast(I32))
 
         def load_words(name, words, slot=None):
             tile = sbuf(name, [P, T], I32, slot)
@@ -84,8 +84,8 @@ def tile_attend_mlpb_swiglu_topk_kernel(tc, qT, k_words, k_scales, c_words, c_sc
         ident = keep.tile([P, P], F32, name="ident")
         make_identity(nc, ident[:])
 
-        load_scales(k_sc_all, k_scales)
-        load_scales(c_sc_all, c_scales)
+        load_scales(k_sc_all, k_scales, nc.scalar)
+        load_scales(c_sc_all, c_scales, nc.sync)
         q_raw = sbuf("q_raw", [P, PACK, NQ], F32, "slot_q")
         nc.sync.dma_start(q_raw[:], qT[0].rearrange("(p j) q -> p j q", j=PACK))
         nc.sync.dma_start(nb_all[P - 1 : P, :], nb[0:1, :])
@@ -165,23 +165,22 @@ def tile_attend_mlpb_swiglu_topk_kernel(tc, qT, k_words, k_scales, c_words, c_sc
                 nc.gpsimd.tensor_scalar(
                     out=scaled[:, t, :], in0=gated[:], scalar1=cols[:, t, 0:1], scalar2=0.0, op0=ALU.mult, op1=ALU.add
                 )
-        staged = sbuf("staged", [P, 3 * P, PACK], BF16)
+        staged = sbuf("staged", [P, HALF + 3 * P, PACK], BF16)
         v_last = sbuf("v_last", [P, P, PACK], BF16, "slot_last")
-        v_bf = [staged[:, blocks[j], :] for j in range(3)] + [v_last[:]]
+        v_bf = [staged[:, HALF + j * P : HALF + (j + 1) * P, :] for j in range(3)] + [v_last[:]]
         y_rows = sbuf("y_rows", [P, PACK, HALF], BF16)
 
-        gated = [sbuf("gated%d" % u, [P, 2, HALF], F32) for u in range(2)]
-        for u in range(2):
-            a_ps = scores(k_codes, k_plane, 1, u, 2 + u, "a_ps")
-            for h in range(2):
-                nc.scalar.activation(gated[u][:, h, :], a_ps[:, h, :], ACT.Silu, bias=cols[:, 2 * u + h, 1:2])
 
         def second_half(u, slot):
+            a_ps = scores(k_codes, k_plane, 1, u, 2 + u, "a_ps")
             z_ps = scores(c_codes, c_plane, 1, u, PACK + 2 + u, "z_ps")
+            gated = sbuf("gated%d" % u, [P, 2, HALF], F32)
             layer = sbuf("layer%d" % u, [P, 2, HALF], F32, slot)
             for h in range(2):
+                nc.scalar.activation(gated[:, h, :], a_ps[:, h, :], ACT.Silu, bias=cols[:, 2 * u + h, 1:2])
+            for h in range(2):
                 nc.scalar.activation(layer[:, h, :], z_ps[:, h, :], ACT.Copy, scale=cols[:, 2 * u + h, 0:1])
-            nc.gpsimd.tensor_tensor(y_rows[:, 2 * u : 2 * u + 2, :], layer[:], gated[u][:], ALU.mult)
+            nc.gpsimd.tensor_tensor(y_rows[:, 2 * u : 2 * u + 2, :], layer[:], gated[:], ALU.mult)
 
         yv_plane = sbuf("yv_plane", [P, NQ + DV], U8)
         y_plane = yv_plane[:, 0:NQ]
@@ -207,7 +206,7 @@ def tile_attend_mlpb_swiglu_topk_kernel(tc, qT, k_words, k_scales, c_words, c_sc
         turned0 = turn_values(0)
         second_half(1, "slot_l0")
         stage_values(0, turned0)
-        y_bf = sbuf("y_bf", [P, NQ, PACK], BF16, "slot_v0")
+        y_bf = sbuf("y_bf", [P, HALF, PACK], BF16, "slot_v0")
         for b in range(2):
             z_ps = bank(PACK + b, [P, PACK, P], "z_ps")
             for t in range(PACK):
@@ -218,12 +217,12 @@ def tile_attend_mlpb_swiglu_topk_kernel(tc, qT, k_words, k_scales, c_words, c_sc
                 scaled[:, :, blocks[b]].rearrange("p t (c i) -> p c t i", i=2),
                 ALU.mult,
             )
-        interleave(y_bf[:, halves[1], :], y_rows[:])
+        interleave(staged[:, 0:HALF, :], y_rows[:])
         gather_values(1)
 
         out_view = out[0].rearrange("(b p) e -> p b e", p=P)
 
-        def multiply(cols, codes, rows, index, engine_copy, res=None):
+        def multiply(cols, codes, rows, index, engine_copy, res=None, queue=nc.sync):
             width = cols.stop - cols.start
             count = rows.stop - rows.start
             o_ps = bank(index, [P, count, width], "o_ps")
@@ -233,24 +232,24 @@ def tile_attend_mlpb_swiglu_topk_kernel(tc, qT, k_words, k_scales, c_words, c_sc
             if res is None:
                 res = sbuf("res%d_%d" % (cols.start, rows.start), [P, count, width], F32)[:]
             engine_copy(res, o_ps[:])
-            nc.sync.dma_start(out_view[:, rows, cols], res)
+            queue.dma_start(out_view[:, rows, cols], res)
 
+        y_first = sbuf("y_first", [P, HALF], U32, "slot_v1")
+        quantize(y_first[:], y_plane[:, halves[0]], y_bf[:])
         gather_values(2)
         first = slice(0, 2 * P)
-        late = sbuf("late", [P, NQ + 2 * P], U32, "slot_v2")
-        y_codes = [late[:, halves[0]], late[:, halves[1]]]
-        codes01 = late[:, NQ : NQ + 2 * P]
-        quantize(late[:, 0:NQ], y_plane, y_bf[:])
-        quantize(codes01, v_plane[:, first], staged[:, first, :])
+        late = sbuf("late", [P, 2 * HALF], U32, "slot_v2")
+        y_codes = [y_first[:], late[:, halves[0]]]
+        codes01 = late[:, halves[1]]
+        quantize(late[:], yv_plane[:, HALF : 3 * HALF], staged[:, 0 : 2 * HALF, :])
         multiply(first, codes01, slice(0, 2), 4, nc.scalar.copy)
         multiply(first, codes01, slice(2, 4), 5, nc.scalar.copy)
         gather_values(3)
         codes2 = sbuf("v_codes2", [P, P], U32, "slot_v3")
         quantize(codes2[:], v_plane[:, blocks[2]], v_bf[2])
         multiply(blocks[2], codes2[:], slice(0, 2), 6, nc.scalar.copy)
+        multiply(blocks[2], codes2[:], slice(2, 4), 1, nc.scalar.copy)
         codes3 = sbuf("v_codes3", [P, P], U32)
         quantize(codes3[:], v_plane[:, blocks[3]], v_bf[3])
-        held = sbuf("held", [P, 2, P], F32, "slot_last")
-        multiply(blocks[2], codes2[:], slice(2, 4), 1, nc.vector.tensor_copy, held[:])
         multiply(blocks[3], codes3[:], slice(0, 2), 7, nc.vector.tensor_copy)
-        multiply(blocks[3], codes3[:], slice(2, 4), 0, nc.scalar.copy)
+        multiply(blocks[3], codes3[:], slice(2, 4), 0, nc.scalar.copy, None, nc.scalar)

@@ -23,7 +23,10 @@ D = 512
 DV = 512
 HALF = NQ // 2
 ROWS = 16
-AHEAD = 3 * T // 4
+AHEAD = T // 2
+SPLIT = 18
+SPLIT_EARLY = 10
+SPLIT_LATE = 14
 FLOPS = 2 * N * NQ * (2 * D + DV)
 BYTES = 4 * D * NQ + 2 * (D * T + D * T // 32) + 4 * DV * T + 4 * T + 4 * N + 2 * N + 4 * NQ * DV
 
@@ -32,10 +35,14 @@ def tile_attend_mlpb_swiglu_topk_kernel(tc, qT, k_words, k_scales, c_words, c_sc
     nc = tc.nc
     with ExitStack() as ctx:
         keep = ctx.enter_context(tc.tile_pool(name="keep", bufs=1))
+        values = ctx.enter_context(tc.tile_pool(name="values", bufs=1))
         psum = ctx.enter_context(tc.psum_pool(name="psum", bufs=1))
 
         def sbuf(name, shape, dtype, slot=None):
             return keep.tile(shape, dtype, name=name, tag=slot or name, align_bytes=64)
+
+        def after(j, at, name, shape, dtype):
+            return values.tile(shape, dtype, name=name, align_bytes=64, offset=4 * T * j + at)
 
         def bank(index, shape, name):
             return psum.tile(shape, F32, name=name, tag="bank%d" % index)
@@ -49,7 +56,7 @@ def tile_attend_mlpb_swiglu_topk_kernel(tc, qT, k_words, k_scales, c_words, c_sc
             return tile
 
         def load_values(j):
-            tile = sbuf("v_all%d" % j, [P, T], F32, "slot_v%d" % j)
+            tile = after(j, 0, "v_all%d" % j, [P, T], F32)
             nc.sync.dma_start(tile[:], vT[j * P : (j + 1) * P, :])
             return tile
 
@@ -81,14 +88,17 @@ def tile_attend_mlpb_swiglu_topk_kernel(tc, qT, k_words, k_scales, c_words, c_sc
         nc.vector.memset(warm[:, 0:1], 0.0)
         nc.vector.memset(nb_all[0 : P - 1, 0 : T // 2], 0.0)
         nc.gpsimd.memset(nb_all[0 : P - 1, T // 2 : T], 0.0)
+        planes = sbuf("planes", [P, 2, PACK, P], U8)
+        plane_words = planes[:].rearrange("p s t m -> p (s t m)").bitcast(I32)
+        nc.gpsimd.memset(plane_words, 0)
         ident = keep.tile([P, P], F32, name="ident")
         make_identity(nc, ident[:])
 
         load_scales(k_sc_all, k_scales, nc.scalar)
         load_scales(c_sc_all, c_scales, nc.sync)
+        nc.sync.dma_start(nb_all[P - 1 : P, :], nb[0:1, :])
         q_raw = sbuf("q_raw", [P, PACK, NQ], F32, "slot_q")
         nc.sync.dma_start(q_raw[:], qT[0].rearrange("(p j) q -> p j q", j=PACK))
-        nc.sync.dma_start(nb_all[P - 1 : P, :], nb[0:1, :])
         nc.sync.dma_start(us_row[:], us[0].rearrange("i o -> o i"))
         k_all = load_words("k_all", k_words, "slot_k")
         c_all = sbuf("c_all", [P, T], I32)
@@ -96,160 +106,150 @@ def tile_attend_mlpb_swiglu_topk_kernel(tc, qT, k_words, k_scales, c_words, c_sc
         nc.sync.dma_start(c_all[:, 0:AHEAD], c_view[:, 0:AHEAD])
         nc.scalar.activation(warm[:, 1:2], warm[:, 0:1], ACT.Silu)
 
-        def gather_scales(window, name):
-            listed = sbuf(name + "_listed", [P, N], U8)
-            nc.vector.tensor_copy(listed[:], window[:].indirect(offsets[:]))
-            return listed
-
-        listed_scales = [gather_scales(k_sc_all, "k"), gather_scales(c_sc_all, "c")]
-        planes = sbuf("planes", [P, 2, PACK, P], U8, "slot_cs")
-        plane_words = planes[:].rearrange("p s t m -> p (s t m)").bitcast(I32)
+        listed_planes = sbuf("listed_planes", [P, 2, PACK, P], U8)
+        for side, window in enumerate((k_sc_all, c_sc_all)):
+            nc.vector.tensor_copy(listed_planes[:, side].rearrange("p t m -> p m t"), window[:].indirect(offsets[:]))
+        listed_words = listed_planes[:].rearrange("p s t m -> p (s t m)").bitcast(I32)
         k_plane = planes[:, 0]
         c_plane = planes[:, 1]
-        for side in range(2):
-            nc.vector.tensor_copy(
-                plane_words[:, side * P : (side + 1) * P].rearrange("p (t m) -> p t m", t=PACK),
-                listed_scales[side][:].bitcast(I32).rearrange("p (m t) -> p t m", t=PACK),
-            )
 
-        def gather_words(window, name, dtype):
-            words = sbuf(name, [P, PACK, P], dtype)
-            nc.vector.tensor_copy(
-                words[:].bitcast(U32).rearrange("p t (m b) -> p m t b", b=RUN), window[:].bitcast(U32).indirect(offsets[:])
-            )
+        def gather_words(window, name):
+            words = sbuf(name, [P, PACK, P], U32)
+            nc.vector.tensor_copy(words[:].rearrange("p t m -> p m t"), window[:].bitcast(U32).indirect(offsets[:]))
             return words
 
         for r in range(4):
-            nc.sync.dma_start(plane_words[r:P:32, :], plane_words[P - ROWS + r : P : 4, :])
+            nc.sync.dma_start(plane_words[r:P:32, :], listed_words[P - ROWS + r : P : 4, :])
         nc.sync.dma_start(c_all[:, AHEAD:T], c_view[:, AHEAD:T])
-        rows = gather_words(nb_all, "rows", F32)
+        rows = sbuf("rows", [P, N], F32)
+        nc.scalar.activation(rows[:], nb_all[:].indirect(offsets[:]), ACT.Copy)
         v_all = [load_values(j) for j in range(DV // P)]
 
         q_bf = [sbuf("q_bf%d" % g, [P, HALF, PACK], BF16) for g in range(2)]
         q_plane = sbuf("q_plane", [P, NQ], U8)
         for g in range(2):
             interleave(q_bf[g][:], q_raw[:, :, halves[g]])
-        nc.scalar.copy(
-            rows[0:1].rearrange("p t (m b) -> p t m b", b=RUN), us_row[:].rearrange("p (m t b) -> p t m b", t=PACK, b=RUN)
-        )
+        nc.vector.tensor_copy(rows[0:1, :], us_row[:])
         rows_ps = bank(4, [P, PACK, P], "rows_ps")
         for t in range(PACK):
-            nc.tensor.transpose(rows_ps[:, t, :], rows[:, t, :], ident[:])
+            nc.tensor.transpose(rows_ps[:, t, :], rows[:, t:N:PACK], ident[:])
         cols = sbuf("cols", [P, PACK, 2], F32, "slot_q")
         nc.scalar.copy(cols[:], rows_ps[:, :, 0 : P : P - 1])
 
         q_codes = [sbuf("q_codes0", [P, HALF], U32, "slot_nb")]
         quantize(q_codes[0][:], q_plane[:, halves[0]], q_bf[0][:])
-        k_codes = gather_words(k_all, "k_codes", U32)
+        k_codes = gather_words(k_all, "k_codes")
         q_codes.append(sbuf("q_codes1", [P, HALF], U32, "slot_k"))
         quantize(q_codes[1][:], q_plane[:, halves[1]], q_bf[1][:])
-        c_codes = gather_words(c_all, "c_codes", U32)
+        c_codes = gather_words(c_all, "c_codes")
 
-        def scores(codes, plane, g, u, index, name):
-            acc = bank(index, [P, 2, HALF], name)
-            for h in range(2):
-                matmul(acc[:, h, :], codes[:, 2 * u + h, :], plane[:, 2 * u + h, :], q_codes[g][:], q_plane[:, halves[g]])
-            return acc
-
-        def gate(g, t, scores_t):
-            tile = sbuf("gate%d%d" % (g, t), [P, HALF], F32)
-            nc.scalar.activation(tile[:], scores_t, ACT.Silu, bias=cols[:, t, 1:2])
-            return tile
-
-        scaled = sbuf("scaled", [P, PACK, HALF], F32)
-        for u in range(2):
-            a_ps = scores(k_codes, k_plane, 0, u, u, "a_ps")
-            for h in range(2):
-                t = 2 * u + h
-                gated = gate(0, t, a_ps[:, h, :])
+        gated = [sbuf("gated%d" % g, [P, PACK, HALF], F32) for g in range(2)]
+        scaled = [sbuf("scaled%d" % g, [P, PACK, HALF], F32) for g in range(2)]
+        for g in range(2):
+            for u in range(2):
+                a_ps = bank(2 * g + u, [P, 2, HALF], "a_ps")
+                for h in range(2):
+                    t = 2 * u + h
+                    matmul(a_ps[:, h, :], k_codes[:, t, :], k_plane[:, t, :], q_codes[g][:], q_plane[:, halves[g]])
+                for h in range(2):
+                    t = 2 * u + h
+                    nc.scalar.activation(gated[g][:, t, :], a_ps[:, h, :], ACT.Silu, bias=cols[:, t, 1:2])
+        for g in range(2):
+            for t in range(2):
                 nc.gpsimd.tensor_scalar(
-                    out=scaled[:, t, :], in0=gated[:], scalar1=cols[:, t, 0:1], scalar2=0.0, op0=ALU.mult, op1=ALU.add
+                    out=scaled[g][:, t, :], in0=gated[g][:, t, :], scalar1=cols[:, t, 0:1], scalar2=0.0, op0=ALU.mult, op1=ALU.add
                 )
-        staged = sbuf("staged", [P, HALF + 3 * P, PACK], BF16)
-        v_last = sbuf("v_last", [P, P, PACK], BF16, "slot_last")
-        v_bf = [staged[:, HALF + j * P : HALF + (j + 1) * P, :] for j in range(3)] + [v_last[:]]
-        y_rows = sbuf("y_rows", [P, PACK, HALF], BF16)
+        for t in range(2, PACK):
+            nc.vector.tensor_scalar(out=scaled[0][:, t, :], in0=gated[0][:, t, :], scalar1=cols[:, t, 0:1], scalar2=None, op0=ALU.mult)
+            nc.scalar.activation(scaled[1][:, t, :], gated[1][:, t, :], ACT.Copy, scale=cols[:, t, 0:1])
 
+        z_ps = []
+        for b in range(NQ // P):
+            g, within = divmod(b, 2)
+            z_ps.append(bank(PACK + b, [P, PACK, P], "z_ps"))
+            for t in range(PACK):
+                matmul(z_ps[b][:, t, :], c_codes[:, t, :], c_plane[:, t, :], q_codes[g][:, blocks[within]], q_plane[:, blocks[b]])
 
-        def second_half(u, slot):
-            a_ps = scores(k_codes, k_plane, 1, u, 2 + u, "a_ps")
-            z_ps = scores(c_codes, c_plane, 1, u, PACK + 2 + u, "z_ps")
-            gated = sbuf("gated%d" % u, [P, 2, HALF], F32)
-            layer = sbuf("layer%d" % u, [P, 2, HALF], F32, slot)
-            for h in range(2):
-                nc.scalar.activation(gated[:, h, :], a_ps[:, h, :], ACT.Silu, bias=cols[:, 2 * u + h, 1:2])
-            for h in range(2):
-                nc.scalar.activation(layer[:, h, :], z_ps[:, h, :], ACT.Copy, scale=cols[:, 2 * u + h, 0:1])
-            nc.gpsimd.tensor_tensor(y_rows[:, 2 * u : 2 * u + 2, :], layer[:], gated[:], ALU.mult)
+        def gather_values(j, share):
+            listed = sbuf("v_listed%d" % j, [P, N], BF16)
+            if share > 0:
+                nc.vector.tensor_copy(listed[:, 0 : 16 * share], v_all[j][:].indirect(offsets[:, 0:share]))
+            if share < N // 16:
+                nc.scalar.activation(listed[:, 16 * share : N], v_all[j][:].indirect(offsets[:, share : N // 16]), ACT.Copy)
+            return listed
 
-        yv_plane = sbuf("yv_plane", [P, NQ + DV], U8)
-        y_plane = yv_plane[:, 0:NQ]
-        v_plane = yv_plane[:, NQ : NQ + DV]
-
-        def turn_values(j):
-            listed = sbuf("v_listed%d" % j, [P, 2, P, 2], BF16, "slot_l%d" % j)
-            nc.vector.tensor_copy(listed[:].rearrange("e u (m b) h -> e m u h b", b=RUN), v_all[j][:].indirect(offsets[:]))
-            words = listed[:].rearrange("e u m h -> e (u m h)").bitcast(F32)
+        def turn_values(j, listed, staged):
+            words = listed[:].bitcast(F32)
             turned = bank(j, [P, 2, P], "v_turned")
             for u in range(2):
-                nc.tensor.transpose(turned[:, u, :], words[:, u * P : (u + 1) * P], ident[:])
-            return turned
-
-        def stage_values(j, turned):
-            dst = v_bf[j].rearrange("p e t -> p (e t)").bitcast(F32)
+                nc.tensor.transpose(turned[:, u, :], words[:, u : N // 2 : 2], ident[:])
+            dst = staged[:].rearrange("p e t -> p (e t)").bitcast(F32)
             nc.scalar.copy(dst.rearrange("p (e u) -> p e u", u=2), turned[:].rearrange("p u e -> p e u"))
 
-        def gather_values(j):
-            stage_values(j, turn_values(j))
+        y_bf = sbuf("y_bf", [P, NQ, PACK], BF16)
 
-        second_half(0, None)
-        turned0 = turn_values(0)
-        second_half(1, "slot_l0")
-        stage_values(0, turned0)
-        y_bf = sbuf("y_bf", [P, HALF, PACK], BF16, "slot_v0")
-        for b in range(2):
-            z_ps = bank(PACK + b, [P, PACK, P], "z_ps")
-            for t in range(PACK):
-                matmul(z_ps[:, t, :], c_codes[:, t, :], c_plane[:, t, :], q_codes[0][:, blocks[b]], q_plane[:, blocks[b]])
-            nc.vector.tensor_tensor(
-                y_bf[:, blocks[b], :].rearrange("p (c i) t -> p c t i", i=2),
-                z_ps[:].rearrange("p t (c i) -> p c t i", i=2),
-                scaled[:, :, blocks[b]].rearrange("p t (c i) -> p c t i", i=2),
-                ALU.mult,
-            )
-        interleave(staged[:, 0:HALF, :], y_rows[:])
-        gather_values(1)
+        def products(g):
+            for within in range(2):
+                b = 2 * g + within
+                nc.vector.tensor_tensor(
+                    y_bf[:, blocks[b], :].rearrange("p (c i) t -> p c t i", i=2),
+                    z_ps[b][:].rearrange("p t (c i) -> p c t i", i=2),
+                    scaled[g][:, :, blocks[within]].rearrange("p t (c i) -> p c t i", i=2),
+                    ALU.mult,
+                )
+
+        products(0)
+        listed = [gather_values(0, SPLIT)]
+        products(1)
+        listed.append(gather_values(1, SPLIT_EARLY))
+        v_bf = [after(1, 0, "v_bf0", [P, P, PACK], BF16)]
+        turn_values(0, listed[0], v_bf[0])
+        y_codes = after(1, 2048, "y_codes", [P, NQ], U32)
+        y_plane = sbuf("y_plane", [P, NQ], U8)
+        v_plane = sbuf("v_plane", [P, DV], U8)
+        quantize(y_codes[:], y_plane[:], y_bf[:])
 
         out_view = out[0].rearrange("(b p) e -> p b e", p=P)
 
-        def multiply(cols, codes, rows, index, engine_copy, res=None, queue=nc.sync):
-            width = cols.stop - cols.start
-            count = rows.stop - rows.start
-            o_ps = bank(index, [P, count, width], "o_ps")
-            for b in range(count):
-                g, within = divmod(rows.start + b, 2)
-                matmul(o_ps[:, b, :], y_codes[g][:, blocks[within]], y_plane[:, blocks[rows.start + b]], codes, v_plane[:, cols])
-            if res is None:
-                res = sbuf("res%d_%d" % (cols.start, rows.start), [P, count, width], F32)[:]
-            engine_copy(res, o_ps[:])
-            queue.dma_start(out_view[:, rows, cols], res)
+        def multiply(j, codes, sums):
+            for b in range(NQ // P):
+                g, within = divmod(b, 2)
+                matmul(sums[g][:, within, :], y_codes[:, blocks[b]], y_plane[:, blocks[b]], codes[:], v_plane[:, blocks[j]])
 
-        y_first = sbuf("y_first", [P, HALF], U32, "slot_v1")
-        quantize(y_first[:], y_plane[:, halves[0]], y_bf[:])
-        gather_values(2)
-        first = slice(0, 2 * P)
-        late = sbuf("late", [P, 2 * HALF], U32, "slot_v2")
-        y_codes = [y_first[:], late[:, halves[0]]]
-        codes01 = late[:, halves[1]]
-        quantize(late[:], yv_plane[:, HALF : 3 * HALF], staged[:, 0 : 2 * HALF, :])
-        multiply(first, codes01, slice(0, 2), 4, nc.scalar.copy)
-        multiply(first, codes01, slice(2, 4), 5, nc.scalar.copy)
-        gather_values(3)
-        codes2 = sbuf("v_codes2", [P, P], U32, "slot_v3")
-        quantize(codes2[:], v_plane[:, blocks[2]], v_bf[2])
-        multiply(blocks[2], codes2[:], slice(0, 2), 6, nc.scalar.copy)
-        multiply(blocks[2], codes2[:], slice(2, 4), 1, nc.scalar.copy)
-        codes3 = sbuf("v_codes3", [P, P], U32)
-        quantize(codes3[:], v_plane[:, blocks[3]], v_bf[3])
-        multiply(blocks[3], codes3[:], slice(0, 2), 7, nc.vector.tensor_copy)
-        multiply(blocks[3], codes3[:], slice(2, 4), 0, nc.scalar.copy, None, nc.scalar)
+        def store(cols, sums, res, copies, queues):
+            for g in range(2):
+                copies[g](res[:, g], sums[g][:])
+                queues[g].dma_start(out_view[:, 2 * g : 2 * g + 2, cols], res[:, g])
+
+        sums01 = [bank(4 + g, [P, 2, 2 * P], "sums01") for g in range(2)]
+        codes = [sbuf("codes0", [P, P], U32)]
+        quantize(codes[0][:], v_plane[:, blocks[0]], v_bf[0][:])
+        multiply(0, codes[0], [acc[:, :, blocks[0]] for acc in sums01])
+        listed.append(gather_values(2, SPLIT_LATE))
+        v_bf.append(after(2, 0, "v_bf1", [P, P, PACK], BF16))
+        turn_values(1, listed[1], v_bf[1])
+        codes.append(sbuf("codes1", [P, P], U32))
+        quantize(codes[1][:], v_plane[:, blocks[1]], v_bf[1][:])
+        multiply(1, codes[1], [acc[:, :, blocks[1]] for acc in sums01])
+        listed.append(gather_values(3, SPLIT))
+        v_bf.append(after(3, 0, "v_bf2", [P, P, PACK], BF16))
+        turn_values(2, listed[2], v_bf[2])
+        res01 = after(3, 2048, "res01", [P, 2, 2, 2 * P], F32)
+        nc.vector.tensor_copy(res01[:, 0], sums01[0][:])
+        nc.sync.dma_start(out_view[:, 0:2, halves[0]], res01[:, 0])
+        codes.append(sbuf("codes2", [P, P], U32))
+        quantize(codes[2][:], v_plane[:, blocks[2]], v_bf[2][:])
+        nc.vector.tensor_copy(res01[:, 1], sums01[1][:])
+        nc.sync.dma_start(out_view[:, 2:4, halves[0]], res01[:, 1])
+        v_bf.append(sbuf("v_bf3", [P, P, PACK], BF16))
+        turn_values(3, listed[3], v_bf[3])
+        sums = [bank(6 + g, [P, 2, P], "sums") for g in range(2)]
+        multiply(2, codes[2], sums)
+        codes.append(sbuf("codes3", [P, P], U32))
+        quantize(codes[3][:], v_plane[:, blocks[3]], v_bf[3][:])
+        res2 = sbuf("res2", [P, 2, 2, P], F32)
+        store(blocks[2], sums, res2, (nc.scalar.copy, nc.scalar.copy), (nc.sync, nc.sync))
+        sums = [bank(g, [P, 2, P], "sums") for g in range(2)]
+        multiply(3, codes[3], sums)
+        res3 = sbuf("res3", [P, 2, 2, P], F32)
+        store(blocks[3], sums, res3, (nc.vector.tensor_copy, nc.scalar.copy), (nc.sync, nc.scalar))

@@ -26,7 +26,6 @@ ROWS = 16
 AHEAD = T // 2
 SPLIT = 18
 SPLIT_EARLY = 10
-SPLIT_LATE = 14
 FLOPS = 2 * N * NQ * (2 * D + DV)
 BYTES = 4 * D * NQ + 2 * (D * T + D * T // 32) + 4 * DV * T + 4 * T + 4 * N + 2 * N + 4 * NQ * DV
 
@@ -96,7 +95,7 @@ def tile_attend_mlpb_swiglu_topk_kernel(tc, qT, k_words, k_scales, c_words, c_sc
 
         load_scales(k_sc_all, k_scales, nc.scalar)
         load_scales(c_sc_all, c_scales, nc.sync)
-        nc.sync.dma_start(nb_all[P - 1 : P, :], nb[0:1, :])
+        nc.scalar.dma_start(nb_all[P - 1 : P, :], nb[0:1, :])
         q_raw = sbuf("q_raw", [P, PACK, NQ], F32, "slot_q")
         nc.sync.dma_start(q_raw[:], qT[0].rearrange("(p j) q -> p j q", j=PACK))
         nc.sync.dma_start(us_row[:], us[0].rearrange("i o -> o i"))
@@ -146,14 +145,10 @@ def tile_attend_mlpb_swiglu_topk_kernel(tc, qT, k_words, k_scales, c_words, c_sc
         gated = [sbuf("gated%d" % g, [P, PACK, HALF], F32) for g in range(2)]
         scaled = [sbuf("scaled%d" % g, [P, PACK, HALF], F32) for g in range(2)]
         for g in range(2):
-            for u in range(2):
-                a_ps = bank(2 * g + u, [P, 2, HALF], "a_ps")
-                for h in range(2):
-                    t = 2 * u + h
-                    matmul(a_ps[:, h, :], k_codes[:, t, :], k_plane[:, t, :], q_codes[g][:], q_plane[:, halves[g]])
-                for h in range(2):
-                    t = 2 * u + h
-                    nc.scalar.activation(gated[g][:, t, :], a_ps[:, h, :], ACT.Silu, bias=cols[:, t, 1:2])
+            for t in range(PACK):
+                a_ps = bank(PACK * g + t, [P, HALF], "a_ps")
+                matmul(a_ps[:], k_codes[:, t, :], k_plane[:, t, :], q_codes[g][:], q_plane[:, halves[g]])
+                nc.scalar.activation(gated[g][:, t, :], a_ps[:], ACT.Silu, bias=cols[:, t, 1:2])
         for g in range(2):
             for t in range(2):
                 nc.gpsimd.tensor_scalar(
@@ -166,7 +161,7 @@ def tile_attend_mlpb_swiglu_topk_kernel(tc, qT, k_words, k_scales, c_words, c_sc
         z_ps = []
         for b in range(NQ // P):
             g, within = divmod(b, 2)
-            z_ps.append(bank(PACK + b, [P, PACK, P], "z_ps"))
+            z_ps.append(bank(b, [P, PACK, P], "z_ps"))
             for t in range(PACK):
                 matmul(z_ps[b][:, t, :], c_codes[:, t, :], c_plane[:, t, :], q_codes[g][:, blocks[within]], q_plane[:, blocks[b]])
 
@@ -180,7 +175,7 @@ def tile_attend_mlpb_swiglu_topk_kernel(tc, qT, k_words, k_scales, c_words, c_sc
 
         def turn_values(j, listed, staged):
             words = listed[:].bitcast(F32)
-            turned = bank(j, [P, 2, P], "v_turned")
+            turned = bank(PACK + j, [P, 2, P], "v_turned")
             for u in range(2):
                 nc.tensor.transpose(turned[:, u, :], words[:, u : N // 2 : 2], ident[:])
             dst = staged[:].rearrange("p e t -> p (e t)").bitcast(F32)
@@ -221,35 +216,32 @@ def tile_attend_mlpb_swiglu_topk_kernel(tc, qT, k_words, k_scales, c_words, c_sc
                 copies[g](res[:, g], sums[g][:])
                 queues[g].dma_start(out_view[:, 2 * g : 2 * g + 2, cols], res[:, g])
 
-        sums01 = [bank(4 + g, [P, 2, 2 * P], "sums01") for g in range(2)]
-        codes = [sbuf("codes0", [P, P], U32)]
+        sums01 = [bank(g, [P, 2, 2 * P], "sums01") for g in range(2)]
+        listed.append(gather_values(2, SPLIT))
+        codes = [after(2, 2048, "codes0", [P, P], U32)]
         quantize(codes[0][:], v_plane[:, blocks[0]], v_bf[0][:])
         multiply(0, codes[0], [acc[:, :, blocks[0]] for acc in sums01])
-        listed.append(gather_values(2, SPLIT_LATE))
         v_bf.append(after(2, 0, "v_bf1", [P, P, PACK], BF16))
         turn_values(1, listed[1], v_bf[1])
         codes.append(sbuf("codes1", [P, P], U32))
         quantize(codes[1][:], v_plane[:, blocks[1]], v_bf[1][:])
+        v_bf.append(sbuf("v_bf2", [P, P, PACK], BF16))
+        turn_values(2, listed[2], v_bf[2])
         multiply(1, codes[1], [acc[:, :, blocks[1]] for acc in sums01])
         listed.append(gather_values(3, SPLIT))
-        v_bf.append(after(3, 0, "v_bf2", [P, P, PACK], BF16))
-        turn_values(2, listed[2], v_bf[2])
-        res01 = after(3, 2048, "res01", [P, 2, 2, 2 * P], F32)
-        nc.vector.tensor_copy(res01[:, 0], sums01[0][:])
-        nc.sync.dma_start(out_view[:, 0:2, halves[0]], res01[:, 0])
-        codes.append(sbuf("codes2", [P, P], U32))
+        codes.append(after(3, 0, "codes2", [P, P], U32))
         quantize(codes[2][:], v_plane[:, blocks[2]], v_bf[2][:])
-        nc.vector.tensor_copy(res01[:, 1], sums01[1][:])
-        nc.sync.dma_start(out_view[:, 2:4, halves[0]], res01[:, 1])
+        res01 = after(3, 2048, "res01", [P, 2, 2, 2 * P], F32)
+        store(halves[0], sums01, res01, (nc.scalar.copy, nc.vector.tensor_copy), (nc.sync, nc.sync))
         v_bf.append(sbuf("v_bf3", [P, P, PACK], BF16))
         turn_values(3, listed[3], v_bf[3])
-        sums = [bank(6 + g, [P, 2, P], "sums") for g in range(2)]
+        sums = [bank(2 + g, [P, 2, P], "sums") for g in range(2)]
         multiply(2, codes[2], sums)
         codes.append(sbuf("codes3", [P, P], U32))
         quantize(codes[3][:], v_plane[:, blocks[3]], v_bf[3][:])
         res2 = sbuf("res2", [P, 2, 2, P], F32)
         store(blocks[2], sums, res2, (nc.scalar.copy, nc.scalar.copy), (nc.sync, nc.sync))
-        sums = [bank(g, [P, 2, P], "sums") for g in range(2)]
+        sums = [bank(4 + g, [P, 2, P], "sums") for g in range(2)]
         multiply(3, codes[3], sums)
         res3 = sbuf("res3", [P, 2, 2, P], F32)
         store(blocks[3], sums, res3, (nc.vector.tensor_copy, nc.scalar.copy), (nc.sync, nc.scalar))

@@ -12,6 +12,7 @@ U8 = mybir.dt.uint8
 FP8X4 = mybir.dt.float8_e4m3fn_x4
 ACT = mybir.ActivationFunctionType
 ALU = mybir.AluOpType
+SIZE = {F32: 4, BF16: 2, I32: 4, U32: 4, U8: 1}
 
 P = 128
 PACK = 4
@@ -23,9 +24,9 @@ D = 512
 DV = 512
 HALF = NQ // 2
 ROWS = 16
+COLS = N // 16
 AHEAD = T // 2
-SPLIT = 18
-SPLIT_EARLY = 10
+SHARE = (0, 0, 16, 16)
 FLOPS = 2 * N * NQ * (2 * D + DV)
 BYTES = 4 * D * NQ + 2 * (D * T + D * T // 32) + 4 * DV * T + 4 * T + 4 * N + 2 * N + 4 * NQ * DV
 
@@ -34,30 +35,26 @@ def tile_attend_mlpb_swiglu_topk_kernel(tc, qT, k_words, k_scales, c_words, c_sc
     nc = tc.nc
     with ExitStack() as ctx:
         keep = ctx.enter_context(tc.tile_pool(name="keep", bufs=1))
-        values = ctx.enter_context(tc.tile_pool(name="values", bufs=1))
+        arena = ctx.enter_context(tc.tile_pool(name="arena", bufs=1))
         psum = ctx.enter_context(tc.psum_pool(name="psum", bufs=1))
+        start = {"free": 0}
 
-        def sbuf(name, shape, dtype, slot=None):
-            return keep.tile(shape, dtype, name=name, tag=slot or name, align_bytes=64)
-
-        def after(j, at, name, shape, dtype):
-            return values.tile(shape, dtype, name=name, align_bytes=64, offset=4 * T * j + at)
+        def sbuf(name, shape, dtype, over=None, at=0):
+            size = SIZE[dtype]
+            for extent in shape[1:]:
+                size = size * extent
+            if over is None:
+                start[name] = start["free"]
+                start["free"] = start["free"] + (size + 63) // 64 * 64
+            else:
+                start[name] = start[over] + at
+            return arena.tile(shape, dtype, name=name, align_bytes=64, offset=start[name])
 
         def bank(index, shape, name):
             return psum.tile(shape, F32, name=name, tag="bank%d" % index)
 
-        def load_scales(tile, scales, queue):
-            queue.dma_start(tile[P - ROWS : P, :].bitcast(I32), scales[0].bitcast(I32))
-
-        def load_words(name, words, slot=None):
-            tile = sbuf(name, [P, T], I32, slot)
-            nc.sync.dma_start(tile[:], words[0].rearrange("p t r -> p (t r)").bitcast(I32))
-            return tile
-
-        def load_values(j):
-            tile = after(j, 0, "v_all%d" % j, [P, T], F32)
-            nc.sync.dma_start(tile[:], vT[j * P : (j + 1) * P, :])
-            return tile
+        def words_view(words):
+            return words[0].rearrange("p t r -> p (t r)").bitcast(I32)
 
         def quantize(codes, plane, values):
             nc.vector.quantize_mx(out=codes.bitcast(FP8X4), scales=plane, in_=values.rearrange("p c t -> p (c t)"))
@@ -68,22 +65,19 @@ def tile_attend_mlpb_swiglu_topk_kernel(tc, qT, k_words, k_scales, c_words, c_sc
                 rhs=rhs_codes.bitcast(FP8X4), rhs_scale=rhs_plane, start=True, stop=True,
             )
 
-        def interleave(dst, src):
-            nc.scalar.copy(dst.rearrange("p (c i) t -> p c t i", i=RUN), src.rearrange("p t (c i) -> p c t i", i=RUN))
-
         halves = [slice(h * HALF, (h + 1) * HALF) for h in range(2)]
         blocks = [slice(j * P, (j + 1) * P) for j in range(DV // P)]
 
-        offsets = keep.tile([P, N // 16], U16, name="offsets")
+        offsets = keep.tile([P, COLS], U16, name="offsets")
         nc.sync.dma_start(offsets[:], offs)
 
-        k_sc_all = sbuf("k_sc_all", [P, T], U8)
-        c_sc_all = sbuf("c_sc_all", [P, T], U8, "slot_cs")
-        nb_all = sbuf("nb_all", [P, T], F32, "slot_nb")
+        k_table = sbuf("k_table", [P, T], U8)
+        c_table = sbuf("c_table", [P, T], U8)
+        nb_all = sbuf("nb_all", [P, T], F32)
         us_row = sbuf("us_row", [1, N], F32)
         warm = keep.tile([P, 2], F32, name="warm")
-        nc.vector.memset(k_sc_all[0 : P - ROWS, :].bitcast(I32), 0)
-        nc.vector.memset(c_sc_all[0 : P - ROWS, :].bitcast(I32), 0)
+        nc.vector.memset(k_table[0 : P - ROWS, :].bitcast(I32), 0)
+        nc.vector.memset(c_table[0 : P - ROWS, :].bitcast(I32), 0)
         nc.vector.memset(warm[:, 0:1], 0.0)
         nc.vector.memset(nb_all[0 : P - 1, 0 : T // 2], 0.0)
         nc.gpsimd.memset(nb_all[0 : P - 1, T // 2 : T], 0.0)
@@ -93,52 +87,55 @@ def tile_attend_mlpb_swiglu_topk_kernel(tc, qT, k_words, k_scales, c_words, c_sc
         ident = keep.tile([P, P], F32, name="ident")
         make_identity(nc, ident[:])
 
-        load_scales(k_sc_all, k_scales, nc.scalar)
-        load_scales(c_sc_all, c_scales, nc.sync)
+        nc.scalar.dma_start(k_table[P - ROWS : P, :].bitcast(I32), k_scales[0].bitcast(I32))
+        nc.sync.dma_start(c_table[P - ROWS : P, :].bitcast(I32), c_scales[0].bitcast(I32))
         nc.scalar.dma_start(nb_all[P - 1 : P, :], nb[0:1, :])
-        q_raw = sbuf("q_raw", [P, PACK, NQ], F32, "slot_q")
+        q_raw = sbuf("q_raw", [P, PACK, NQ], F32)
         nc.sync.dma_start(q_raw[:], qT[0].rearrange("(p j) q -> p j q", j=PACK))
         nc.sync.dma_start(us_row[:], us[0].rearrange("i o -> o i"))
-        k_all = load_words("k_all", k_words, "slot_k")
+        k_all = sbuf("k_all", [P, T], I32)
+        nc.sync.dma_start(k_all[:], words_view(k_words))
         c_all = sbuf("c_all", [P, T], I32)
-        c_view = c_words[0].rearrange("p t r -> p (t r)").bitcast(I32)
-        nc.sync.dma_start(c_all[:, 0:AHEAD], c_view[:, 0:AHEAD])
+        nc.sync.dma_start(c_all[:, 0:AHEAD], words_view(c_words)[:, 0:AHEAD])
         nc.scalar.activation(warm[:, 1:2], warm[:, 0:1], ACT.Silu)
 
         listed_planes = sbuf("listed_planes", [P, 2, PACK, P], U8)
-        for side, window in enumerate((k_sc_all, c_sc_all)):
-            nc.vector.tensor_copy(listed_planes[:, side].rearrange("p t m -> p m t"), window[:].indirect(offsets[:]))
+        for side, table in enumerate((k_table, c_table)):
+            nc.vector.tensor_copy(listed_planes[:, side].rearrange("p t m -> p m t"), table[:].indirect(offsets[:]))
         listed_words = listed_planes[:].rearrange("p s t m -> p (s t m)").bitcast(I32)
-        k_plane = planes[:, 0]
-        c_plane = planes[:, 1]
+        for r in range(4):
+            nc.sync.dma_start(plane_words[r:P:32, :], listed_words[P - ROWS + r : P : 4, :])
+        nc.sync.dma_start(c_all[:, AHEAD:T], words_view(c_words)[:, AHEAD:T])
+        v_all = []
+        for j in range(DV // P):
+            v_all.append(sbuf("v_all%d" % j, [P, T], F32))
+            nc.sync.dma_start(v_all[j][:], vT[blocks[j], :])
+
+        rows = sbuf("rows", [P, N], F32)
+        nc.scalar.activation(rows[:], nb_all[:].indirect(offsets[:]), ACT.Copy)
+        q_bf = [sbuf("q_bf%d" % g, [P, HALF, PACK], BF16) for g in range(2)]
+        for g in range(2):
+            nc.scalar.copy(
+                q_bf[g][:].rearrange("p (c i) t -> p c t i", i=RUN),
+                q_raw[:, :, halves[g]].rearrange("p t (c i) -> p c t i", i=RUN),
+            )
+        nc.vector.tensor_copy(rows[0:1, :], us_row[:])
+        rows_ps = bank(4, [P, PACK, P], "rows_ps")
+        for t in range(PACK):
+            nc.tensor.transpose(rows_ps[:, t, :], rows[:, t:N:PACK], ident[:])
+        cols = sbuf("cols", [P, PACK, 2], F32, "q_raw")
+        nc.scalar.copy(cols[:], rows_ps[:, :, 0 : P : P - 1])
 
         def gather_words(window, name):
             words = sbuf(name, [P, PACK, P], U32)
             nc.vector.tensor_copy(words[:].rearrange("p t m -> p m t"), window[:].bitcast(U32).indirect(offsets[:]))
             return words
 
-        for r in range(4):
-            nc.sync.dma_start(plane_words[r:P:32, :], listed_words[P - ROWS + r : P : 4, :])
-        nc.sync.dma_start(c_all[:, AHEAD:T], c_view[:, AHEAD:T])
-        rows = sbuf("rows", [P, N], F32)
-        nc.scalar.activation(rows[:], nb_all[:].indirect(offsets[:]), ACT.Copy)
-        v_all = [load_values(j) for j in range(DV // P)]
-
-        q_bf = [sbuf("q_bf%d" % g, [P, HALF, PACK], BF16) for g in range(2)]
         q_plane = sbuf("q_plane", [P, NQ], U8)
-        for g in range(2):
-            interleave(q_bf[g][:], q_raw[:, :, halves[g]])
-        nc.vector.tensor_copy(rows[0:1, :], us_row[:])
-        rows_ps = bank(4, [P, PACK, P], "rows_ps")
-        for t in range(PACK):
-            nc.tensor.transpose(rows_ps[:, t, :], rows[:, t:N:PACK], ident[:])
-        cols = sbuf("cols", [P, PACK, 2], F32, "slot_q")
-        nc.scalar.copy(cols[:], rows_ps[:, :, 0 : P : P - 1])
-
-        q_codes = [sbuf("q_codes0", [P, HALF], U32, "slot_nb")]
+        q_codes = [sbuf("q_codes0", [P, HALF], U32, "nb_all")]
         quantize(q_codes[0][:], q_plane[:, halves[0]], q_bf[0][:])
         k_codes = gather_words(k_all, "k_codes")
-        q_codes.append(sbuf("q_codes1", [P, HALF], U32, "slot_k"))
+        q_codes.append(sbuf("q_codes1", [P, HALF], U32, "k_all"))
         quantize(q_codes[1][:], q_plane[:, halves[1]], q_bf[1][:])
         c_codes = gather_words(c_all, "c_codes")
 
@@ -147,7 +144,7 @@ def tile_attend_mlpb_swiglu_topk_kernel(tc, qT, k_words, k_scales, c_words, c_sc
         for g in range(2):
             for t in range(PACK):
                 a_ps = bank(PACK * g + t, [P, HALF], "a_ps")
-                matmul(a_ps[:], k_codes[:, t, :], k_plane[:, t, :], q_codes[g][:], q_plane[:, halves[g]])
+                matmul(a_ps[:], k_codes[:, t, :], planes[:, 0, t, :], q_codes[g][:], q_plane[:, halves[g]])
                 nc.scalar.activation(gated[g][:, t, :], a_ps[:], ACT.Silu, bias=cols[:, t, 1:2])
         for g in range(2):
             for t in range(2):
@@ -158,90 +155,75 @@ def tile_attend_mlpb_swiglu_topk_kernel(tc, qT, k_words, k_scales, c_words, c_sc
             nc.vector.tensor_scalar(out=scaled[0][:, t, :], in0=gated[0][:, t, :], scalar1=cols[:, t, 0:1], scalar2=None, op0=ALU.mult)
             nc.scalar.activation(scaled[1][:, t, :], gated[1][:, t, :], ACT.Copy, scale=cols[:, t, 0:1])
 
-        z_ps = []
+        y_bf = [sbuf("y_bf%d" % g, [P, HALF, PACK], BF16) for g in range(2)]
         for b in range(NQ // P):
             g, within = divmod(b, 2)
-            z_ps.append(bank(b, [P, PACK, P], "z_ps"))
+            z_ps = bank(b, [P, PACK, P], "z_ps")
             for t in range(PACK):
-                matmul(z_ps[b][:, t, :], c_codes[:, t, :], c_plane[:, t, :], q_codes[g][:, blocks[within]], q_plane[:, blocks[b]])
+                matmul(z_ps[:, t, :], c_codes[:, t, :], planes[:, 1, t, :], q_codes[g][:, blocks[within]], q_plane[:, blocks[b]])
+            nc.vector.tensor_tensor(
+                y_bf[g][:, blocks[within], :].rearrange("p (c i) t -> p c t i", i=2),
+                z_ps[:].rearrange("p t (c i) -> p c t i", i=2),
+                scaled[g][:, :, blocks[within]].rearrange("p t (c i) -> p c t i", i=2),
+                ALU.mult,
+            )
+        y_codes = sbuf("y_codes", [P, NQ], U32)
+        y_plane = sbuf("y_plane", [P, NQ], U8)
+        v_plane = sbuf("v_plane", [P, DV], U8)
 
-        def gather_values(j, share):
-            listed = sbuf("v_listed%d" % j, [P, N], BF16)
+        def gather_values(j, over=None):
+            listed = sbuf("v_listed%d" % j, [P, N], BF16, over)
+            share = SHARE[j]
             if share > 0:
                 nc.vector.tensor_copy(listed[:, 0 : 16 * share], v_all[j][:].indirect(offsets[:, 0:share]))
-            if share < N // 16:
-                nc.scalar.activation(listed[:, 16 * share : N], v_all[j][:].indirect(offsets[:, share : N // 16]), ACT.Copy)
+            nc.scalar.activation(listed[:, 16 * share : N], v_all[j][:].indirect(offsets[:, share:COLS]), ACT.Copy)
             return listed
 
-        def turn_values(j, listed, staged):
+        def turn_values(j, listed, over=None):
             words = listed[:].bitcast(F32)
             turned = bank(PACK + j, [P, 2, P], "v_turned")
             for u in range(2):
                 nc.tensor.transpose(turned[:, u, :], words[:, u : N // 2 : 2], ident[:])
+            staged = sbuf("v_bf%d" % j, [P, P, PACK], BF16, over)
             dst = staged[:].rearrange("p e t -> p (e t)").bitcast(F32)
             nc.scalar.copy(dst.rearrange("p (e u) -> p e u", u=2), turned[:].rearrange("p u e -> p e u"))
+            return staged
 
-        y_bf = sbuf("y_bf", [P, NQ, PACK], BF16)
-
-        def products(g):
-            for within in range(2):
-                b = 2 * g + within
-                nc.vector.tensor_tensor(
-                    y_bf[:, blocks[b], :].rearrange("p (c i) t -> p c t i", i=2),
-                    z_ps[b][:].rearrange("p t (c i) -> p c t i", i=2),
-                    scaled[g][:, :, blocks[within]].rearrange("p t (c i) -> p c t i", i=2),
-                    ALU.mult,
-                )
-
-        products(0)
-        listed = [gather_values(0, SPLIT)]
-        products(1)
-        listed.append(gather_values(1, SPLIT_EARLY))
-        v_bf = [after(1, 0, "v_bf0", [P, P, PACK], BF16)]
-        turn_values(0, listed[0], v_bf[0])
-        y_codes = after(1, 2048, "y_codes", [P, NQ], U32)
-        y_plane = sbuf("y_plane", [P, NQ], U8)
-        v_plane = sbuf("v_plane", [P, DV], U8)
-        quantize(y_codes[:], y_plane[:], y_bf[:])
+        def multiply(j, staged, sums, over=None, at=0):
+            codes = sbuf("v_codes%d" % j, [P, P], U32, over, at)
+            quantize(codes[:], v_plane[:, blocks[j]], staged[:])
+            for b in range(NQ // P):
+                matmul(sums[b], y_codes[:, blocks[b]], y_plane[:, blocks[b]], codes[:], v_plane[:, blocks[j]])
 
         out_view = out[0].rearrange("(b p) e -> p b e", p=P)
 
-        def multiply(j, codes, sums):
-            for b in range(NQ // P):
-                g, within = divmod(b, 2)
-                matmul(sums[g][:, within, :], y_codes[:, blocks[b]], y_plane[:, blocks[b]], codes[:], v_plane[:, blocks[j]])
+        def store(name, rows_at, cols_at, sums, copy, queue, over=None, at=0):
+            res = sbuf(name, list(sums.shape), F32, over, at)
+            copy(res[:], sums[:, :, :])
+            queue.dma_start(out_view[:, rows_at, cols_at], res[:])
 
-        def store(cols, sums, res, copies, queues):
-            for g in range(2):
-                copies[g](res[:, g], sums[g][:])
-                queues[g].dma_start(out_view[:, 2 * g : 2 * g + 2, cols], res[:, g])
-
-        sums01 = [bank(g, [P, 2, 2 * P], "sums01") for g in range(2)]
-        listed.append(gather_values(2, SPLIT))
-        codes = [after(2, 2048, "codes0", [P, P], U32)]
-        quantize(codes[0][:], v_plane[:, blocks[0]], v_bf[0][:])
-        multiply(0, codes[0], [acc[:, :, blocks[0]] for acc in sums01])
-        v_bf.append(after(2, 0, "v_bf1", [P, P, PACK], BF16))
-        turn_values(1, listed[1], v_bf[1])
-        codes.append(sbuf("codes1", [P, P], U32))
-        quantize(codes[1][:], v_plane[:, blocks[1]], v_bf[1][:])
-        v_bf.append(sbuf("v_bf2", [P, P, PACK], BF16))
-        turn_values(2, listed[2], v_bf[2])
-        multiply(1, codes[1], [acc[:, :, blocks[1]] for acc in sums01])
-        listed.append(gather_values(3, SPLIT))
-        codes.append(after(3, 0, "codes2", [P, P], U32))
-        quantize(codes[2][:], v_plane[:, blocks[2]], v_bf[2][:])
-        res01 = after(3, 2048, "res01", [P, 2, 2, 2 * P], F32)
-        store(halves[0], sums01, res01, (nc.scalar.copy, nc.vector.tensor_copy), (nc.sync, nc.sync))
-        v_bf.append(sbuf("v_bf3", [P, P, PACK], BF16))
-        turn_values(3, listed[3], v_bf[3])
-        sums = [bank(2 + g, [P, 2, P], "sums") for g in range(2)]
-        multiply(2, codes[2], sums)
-        codes.append(sbuf("codes3", [P, P], U32))
-        quantize(codes[3][:], v_plane[:, blocks[3]], v_bf[3][:])
-        res2 = sbuf("res2", [P, 2, 2, P], F32)
-        store(blocks[2], sums, res2, (nc.scalar.copy, nc.scalar.copy), (nc.sync, nc.sync))
-        sums = [bank(4 + g, [P, 2, P], "sums") for g in range(2)]
-        multiply(3, codes[3], sums)
-        res3 = sbuf("res3", [P, 2, 2, P], F32)
-        store(blocks[3], sums, res3, (nc.vector.tensor_copy, nc.scalar.copy), (nc.sync, nc.scalar))
+        listed0 = gather_values(0, "k_codes")
+        for g in range(2):
+            quantize(y_codes[:, halves[g]], y_plane[:, halves[g]], y_bf[g][:])
+        listed1 = gather_values(1)
+        v_bf0 = turn_values(0, listed0, "v_all1")
+        listed2 = gather_values(2)
+        v_bf1 = turn_values(1, listed1, "v_all2")
+        v_bf2 = turn_values(2, listed2)
+        early = [bank(g, [P, 2, 2 * P], "early") for g in range(2)]
+        third = [bank(2 + g, [P, 2, P], "third") for g in range(2)]
+        multiply(0, v_bf0, [early[b // 2][:, b % 2, blocks[0]] for b in range(4)], "v_all2", 2048)
+        multiply(1, v_bf1, [early[b // 2][:, b % 2, blocks[1]] for b in range(4)])
+        listed3 = gather_values(3)
+        copies = (nc.vector.tensor_copy, nc.scalar.copy)
+        v_bf3 = turn_values(3, listed3)
+        multiply(2, v_bf2, [third[b // 2][:, b % 2, :] for b in range(4)], "v_all3", 4096)
+        for b in range(2):
+            store("res_early%d" % b, slice(b, b + 1), halves[0], early[0][:, b : b + 1, :], copies[1], nc.sync, "v_all3", 1024 * b)
+        store("res_early2", slice(2, 4), halves[0], early[1], copies[0], nc.sync, "v_all3", 2048)
+        last = [bank(4 + g, [P, 2, P], "last") for g in range(2)]
+        multiply(3, v_bf3, [last[b // 2][:, b % 2, :] for b in range(4)])
+        for g in range(2):
+            store("res_third%d" % g, slice(2 * g, 2 * g + 2), blocks[2], third[g], copies[1], nc.sync)
+        store("res_last0", slice(0, 2), blocks[3], last[0], copies[0], nc.sync)
+        store("res_last1", slice(2, 4), blocks[3], last[1], copies[1], nc.scalar)

@@ -25,7 +25,7 @@ DV = 512
 HALF = NQ // 2
 ROWS = 16
 COLS = N // 16
-AHEAD = T // 2
+AHEAD = 3 * T // 4
 SHARE = (0, 0, 16, 16)
 FLOPS = 2 * N * NQ * (2 * D + DV)
 BYTES = 4 * D * NQ + 2 * (D * T + D * T // 32) + 4 * DV * T + 4 * T + 4 * N + 2 * N + 4 * NQ * DV
@@ -79,13 +79,7 @@ def tile_attend_mlpb_swiglu_topk_kernel(tc, qT, k_words, k_scales, c_words, c_sc
         nc.vector.memset(k_table[0 : P - ROWS, :].bitcast(I32), 0)
         nc.vector.memset(c_table[0 : P - ROWS, :].bitcast(I32), 0)
         nc.vector.memset(warm[:, 0:1], 0.0)
-        nc.vector.memset(nb_all[0 : P - 1, 0 : T // 2], 0.0)
-        nc.gpsimd.memset(nb_all[0 : P - 1, T // 2 : T], 0.0)
-        planes = sbuf("planes", [P, 2, PACK, P], U8)
-        plane_words = planes[:].rearrange("p s t m -> p (s t m)").bitcast(I32)
-        nc.gpsimd.memset(plane_words, 0)
-        ident = keep.tile([P, P], F32, name="ident")
-        make_identity(nc, ident[:])
+        nc.vector.memset(nb_all[0 : P - 1, :], 0.0)
 
         nc.scalar.dma_start(k_table[P - ROWS : P, :].bitcast(I32), k_scales[0].bitcast(I32))
         nc.sync.dma_start(c_table[P - ROWS : P, :].bitcast(I32), c_scales[0].bitcast(I32))
@@ -102,6 +96,11 @@ def tile_attend_mlpb_swiglu_topk_kernel(tc, qT, k_words, k_scales, c_words, c_sc
         listed_planes = sbuf("listed_planes", [P, 2, PACK, P], U8)
         for side, table in enumerate((k_table, c_table)):
             nc.vector.tensor_copy(listed_planes[:, side].rearrange("p t m -> p m t"), table[:].indirect(offsets[:]))
+        planes = sbuf("planes", [P, 2, PACK, P], U8, "k_table")
+        plane_words = planes[:].rearrange("p s t m -> p (s t m)").bitcast(I32)
+        nc.gpsimd.memset(plane_words, 0)
+        ident = sbuf("ident", [P, P], F32, "k_table", 1024)
+        make_identity(nc, ident[:])
         listed_words = listed_planes[:].rearrange("p s t m -> p (s t m)").bitcast(I32)
         for r in range(4):
             nc.sync.dma_start(plane_words[r:P:32, :], listed_words[P - ROWS + r : P : 4, :])

@@ -193,6 +193,7 @@ def tile_attend_mlpb_swiglu_topk_kernel(tc, qT, k_words, k_scales, c_words, c_sc
             quantize(codes[:], v_plane[:, blocks[j]], staged[:])
             for b in range(NQ // P):
                 matmul(sums[b], y_codes[:, blocks[b]], y_plane[:, blocks[b]], codes[:], v_plane[:, blocks[j]])
+            return codes
 
         out_view = out[0].rearrange("(b p) e -> p b e", p=P)
 
@@ -212,7 +213,9 @@ def tile_attend_mlpb_swiglu_topk_kernel(tc, qT, k_words, k_scales, c_words, c_sc
         early = [bank(g, [P, 2, 2 * P], "early") for g in range(2)]
         third = [bank(2 + g, [P, 2, P], "third") for g in range(2)]
         multiply(0, v_bf0, [early[b // 2][:, b % 2, blocks[0]] for b in range(4)], "v_all2", 2048)
-        multiply(1, v_bf1, [early[b // 2][:, b % 2, blocks[1]] for b in range(4)])
+        codes1 = multiply(1, v_bf1, [early[b // 2][:, b % 2, blocks[1]] for b in range(4)])
+        idle = bank(4, [P, NQ], "idle")
+        matmul(idle[:], codes1[:], v_plane[:, blocks[1]], y_codes[:], y_plane[:])
         listed3 = gather_values(3)
         copies = (nc.vector.tensor_copy, nc.scalar.copy)
         v_bf3 = turn_values(3, listed3)

@@ -207,22 +207,24 @@ def tile_attend_mlpb_swiglu_topk_kernel(tc, qT, k_words, k_scales, c_words, c_sc
             quantize(y_codes[:, halves[g]], y_plane[:, halves[g]], y_bf[g][:])
         listed1 = gather_values(1)
         v_bf0 = turn_values(0, listed0, "v_all1")
+        copies = (nc.vector.tensor_copy, nc.scalar.copy)
+        first = [bank(g, [P, 2, P], "first") for g in range(2)]
+        multiply(0, v_bf0, [first[b // 2][:, b % 2, :] for b in range(4)])
         listed2 = gather_values(2)
         v_bf1 = turn_values(1, listed1, "v_all2")
+        store("res_first0", slice(0, 2), blocks[0], first[0], copies[1], nc.sync, "v_all2", 2048)
         v_bf2 = turn_values(2, listed2)
-        early = [bank(g, [P, 2, 2 * P], "early") for g in range(2)]
-        third = [bank(2 + g, [P, 2, P], "third") for g in range(2)]
-        multiply(0, v_bf0, [early[b // 2][:, b % 2, blocks[0]] for b in range(4)], "v_all2", 2048)
-        codes1 = multiply(1, v_bf1, [early[b // 2][:, b % 2, blocks[1]] for b in range(4)])
+        second = [bank(2 + g, [P, 2, P], "second") for g in range(2)]
+        codes1 = multiply(1, v_bf1, [second[b // 2][:, b % 2, :] for b in range(4)])
+        store("res_first1", slice(2, 4), blocks[0], first[1], copies[0], nc.sync, "v_all2", 3072)
         idle = bank(4, [P, NQ], "idle")
         matmul(idle[:], codes1[:], v_plane[:, blocks[1]], y_codes[:], y_plane[:])
         listed3 = gather_values(3)
-        copies = (nc.vector.tensor_copy, nc.scalar.copy)
         v_bf3 = turn_values(3, listed3)
+        third = [bank(g, [P, 2, P], "third") for g in range(2)]
         multiply(2, v_bf2, [third[b // 2][:, b % 2, :] for b in range(4)], "v_all3", 4096)
-        for b in range(2):
-            store("res_early%d" % b, slice(b, b + 1), halves[0], early[0][:, b : b + 1, :], copies[1], nc.sync, "v_all3", 1024 * b)
-        store("res_early2", slice(2, 4), halves[0], early[1], copies[0], nc.sync, "v_all3", 2048)
+        for g in range(2):
+            store("res_second%d" % g, slice(2 * g, 2 * g + 2), blocks[1], second[g], copies[1 - g], nc.sync, "v_all3", 1024 * g)
         last = [bank(4 + g, [P, 2, P], "last") for g in range(2)]
         multiply(3, v_bf3, [last[b // 2][:, b % 2, :] for b in range(4)])
         for g in range(2):

@@ -193,7 +193,6 @@ def tile_attend_mlpb_swiglu_topk_kernel(tc, qT, k_words, k_scales, c_words, c_sc
             quantize(codes[:], v_plane[:, blocks[j]], staged[:])
             for b in range(NQ // P):
                 matmul(sums[b], y_codes[:, blocks[b]], y_plane[:, blocks[b]], codes[:], v_plane[:, blocks[j]])
-            return codes
 
         out_view = out[0].rearrange("(b p) e -> p b e", p=P)
 
@@ -215,10 +214,8 @@ def tile_attend_mlpb_swiglu_topk_kernel(tc, qT, k_words, k_scales, c_words, c_sc
         store("res_first0", slice(0, 2), blocks[0], first[0], copies[1], nc.sync, "v_all2", 2048)
         v_bf2 = turn_values(2, listed2)
         second = [bank(2 + g, [P, 2, P], "second") for g in range(2)]
-        codes1 = multiply(1, v_bf1, [second[b // 2][:, b % 2, :] for b in range(4)])
+        multiply(1, v_bf1, [second[b // 2][:, b % 2, :] for b in range(4)])
         store("res_first1", slice(2, 4), blocks[0], first[1], copies[0], nc.sync, "v_all2", 3072)
-        idle = bank(4, [P, NQ], "idle")
-        matmul(idle[:], codes1[:], v_plane[:, blocks[1]], y_codes[:], y_plane[:])
         listed3 = gather_values(3)
         v_bf3 = turn_values(3, listed3)
         third = [bank(g, [P, 2, P], "third") for g in range(2)]

@@ -222,9 +222,12 @@ def tile_attend_mlpb_swiglu_topk_kernel(tc, qT, k_words, k_scales, c_words, c_sc
         multiply(2, v_bf2, [third[b // 2][:, b % 2, :] for b in range(4)], "v_all3", 4096)
         for g in range(2):
             store("res_second%d" % g, slice(2 * g, 2 * g + 2), blocks[1], second[g], copies[1 - g], nc.sync, "v_all3", 1024 * g)
-        last = [bank(4 + g, [P, 2, P], "last") for g in range(2)]
-        multiply(3, v_bf3, [last[b // 2][:, b % 2, :] for b in range(4)])
-        for g in range(2):
-            store("res_third%d" % g, slice(2 * g, 2 * g + 2), blocks[2], third[g], copies[1], nc.sync)
-        store("res_last0", slice(0, 2), blocks[3], last[0], copies[0], nc.sync)
-        store("res_last1", slice(2, 4), blocks[3], last[1], copies[1], nc.scalar)
+        last = [bank(index, [P, P], "last") for index in (4, 5, 6, 2)]
+        multiply(3, v_bf3, [tile[:] for tile in last])
+        store("res_third0", slice(0, 2), blocks[2], third[0], copies[1], nc.sync)
+        store("res_third1", slice(2, 4), blocks[2], third[1], copies[0], nc.sync, "v_bf3")
+        for g, queue in enumerate((nc.sync, nc.scalar)):
+            res = sbuf("res_last%d" % g, [P, 2, P], F32)
+            for w in range(2):
+                copies[w](res[:, w, :], last[2 * g + w][:])
+            queue.dma_start(out_view[:, 2 * g : 2 * g + 2, blocks[3]], res[:])

@@ -211,11 +211,13 @@ def tile_attend_mlpb_swiglu_topk_kernel(tc, qT, k_words, k_scales, c_words, c_sc
         multiply(0, v_bf0, [first[b // 2][:, b % 2, :] for b in range(4)])
         listed2 = gather_values(2)
         v_bf1 = turn_values(1, listed1, "v_all2")
-        store("res_first0", slice(0, 2), blocks[0], first[0], copies[1], nc.sync, "v_all2", 2048)
+        res_first = sbuf("res_first", [P, 4, P], F32, "v_all2", 2048)
+        copies[1](res_first[:, 0:2, :], first[0][:])
         v_bf2 = turn_values(2, listed2)
         second = [bank(2 + g, [P, 2, P], "second") for g in range(2)]
         multiply(1, v_bf1, [second[b // 2][:, b % 2, :] for b in range(4)])
-        store("res_first1", slice(2, 4), blocks[0], first[1], copies[0], nc.sync, "v_all2", 3072)
+        copies[0](res_first[:, 2:4, :], first[1][:])
+        nc.sync.dma_start(out_view[:, :, blocks[0]], res_first[:])
         listed3 = gather_values(3)
         v_bf3 = turn_values(3, listed3)
         third = [bank(g, [P, 2, P], "third") for g in range(2)]
@@ -226,8 +228,8 @@ def tile_attend_mlpb_swiglu_topk_kernel(tc, qT, k_words, k_scales, c_words, c_sc
         multiply(3, v_bf3, [tile[:] for tile in last])
         store("res_third0", slice(0, 2), blocks[2], third[0], copies[1], nc.sync)
         store("res_third1", slice(2, 4), blocks[2], third[1], copies[0], nc.sync, "v_bf3")
-        for g, queue in enumerate((nc.sync, nc.scalar)):
+        for g in range(2):
             res = sbuf("res_last%d" % g, [P, 2, P], F32)
             for w in range(2):
                 copies[w](res[:, w, :], last[2 * g + w][:])
-            queue.dma_start(out_view[:, 2 * g : 2 * g + 2, blocks[3]], res[:])
+            nc.sync.dma_start(out_view[:, 2 * g : 2 * g + 2, blocks[3]], res[:])

@@ -25,6 +25,7 @@ DV = 512
 HALF = NQ // 2
 ROWS = 16
 COLS = N // 16
+ALIGN = 256
 AHEAD = 3 * T // 4
 SHARE = (0, 0, 16, 16)
 FLOPS = 2 * N * NQ * (2 * D + DV)
@@ -45,10 +46,10 @@ def tile_attend_mlpb_swiglu_topk_kernel(tc, qT, k_words, k_scales, c_words, c_sc
                 size = size * extent
             if over is None:
                 start[name] = start["free"]
-                start["free"] = start["free"] + (size + 63) // 64 * 64
+                start["free"] = start["free"] + (size + ALIGN - 1) // ALIGN * ALIGN
             else:
                 start[name] = start[over] + at
-            return arena.tile(shape, dtype, name=name, align_bytes=64, offset=start[name])
+            return arena.tile(shape, dtype, name=name, align_bytes=ALIGN, offset=start[name])
 
         def bank(index, shape, name):
             return psum.tile(shape, F32, name=name, tag="bank%d" % index)

from contextlib import ExitStack

import concourse.mybir as mybir
from concourse.masks import make_identity

F32 = mybir.dt.float32
BF16 = mybir.dt.bfloat16
I32 = mybir.dt.int32
U32 = mybir.dt.uint32
U16 = mybir.dt.uint16
U8 = mybir.dt.uint8
FP8X4 = mybir.dt.float8_e4m3fn_x4
ACT = mybir.ActivationFunctionType
ALU = mybir.AluOpType
SIZE = {F32: 4, BF16: 2, I32: 4, U32: 4, U8: 1}

P = 128
PACK = 4
RUN = 4
T = 2048
N = 512
NQ = 512
D = 512
DV = 512
HALF = NQ // 2
ROWS = 16
COLS = N // 16
ALIGN = 256
AHEAD = 3 * T // 4
SHARE = (0, 0, 16, 16)
FLOPS = 2 * N * NQ * (2 * D + DV)
BYTES = 4 * D * NQ + 2 * (D * T + D * T // 32) + 4 * DV * T + 4 * T + 4 * N + 2 * N + 4 * NQ * DV


def tile_attend_mlpb_swiglu_topk_kernel(tc, qT, k_words, k_scales, c_words, c_scales, vT, nb, us, offs, out):
    nc = tc.nc
    with ExitStack() as ctx:
        keep = ctx.enter_context(tc.tile_pool(name="keep", bufs=1))
        arena = ctx.enter_context(tc.tile_pool(name="arena", bufs=1))
        psum = ctx.enter_context(tc.psum_pool(name="psum", bufs=1))
        start = {"free": 0}

        def sbuf(name, shape, dtype, over=None, at=0):
            size = SIZE[dtype]
            for extent in shape[1:]:
                size = size * extent
            if over is None:
                start[name] = start["free"]
                start["free"] = start["free"] + (size + ALIGN - 1) // ALIGN * ALIGN
            else:
                start[name] = start[over] + at
            return arena.tile(shape, dtype, name=name, align_bytes=ALIGN, offset=start[name])

        def bank(index, shape, name):
            return psum.tile(shape, F32, name=name, tag="bank%d" % index)

        def words_view(words):
            return words[0].rearrange("p t r -> p (t r)").bitcast(I32)

        def quantize(codes, plane, values):
            nc.vector.quantize_mx(out=codes.bitcast(FP8X4), scales=plane, in_=values.rearrange("p c t -> p (c t)"))

        def matmul(acc, lhs_codes, lhs_plane, rhs_codes, rhs_plane):
            nc.tensor.matmul_mx(
                out=acc, lhsT=lhs_codes.bitcast(FP8X4), lhsT_scale=lhs_plane,
                rhs=rhs_codes.bitcast(FP8X4), rhs_scale=rhs_plane, start=True, stop=True,
            )

        halves = [slice(h * HALF, (h + 1) * HALF) for h in range(2)]
        blocks = [slice(j * P, (j + 1) * P) for j in range(DV // P)]

        offsets = keep.tile([P, COLS], U16, name="offsets")
        nc.sync.dma_start(offsets[:], offs)

        k_table = sbuf("k_table", [P, T], U8)
        c_table = sbuf("c_table", [P, T], U8)
        nb_all = sbuf("nb_all", [P, T], F32)
        us_row = sbuf("us_row", [1, N], F32)
        warm = keep.tile([P, 2], F32, name="warm")
        nc.vector.memset(k_table[0 : P - ROWS, :].bitcast(I32), 0)
        nc.vector.memset(c_table[0 : P - ROWS, :].bitcast(I32), 0)
        nc.vector.memset(warm[:, 0:1], 0.0)
        nc.vector.memset(nb_all[0 : P - 1, :], 0.0)

        nc.scalar.dma_start(k_table[P - ROWS : P, :].bitcast(I32), k_scales[0].bitcast(I32))
        nc.sync.dma_start(c_table[P - ROWS : P, :].bitcast(I32), c_scales[0].bitcast(I32))
        nc.scalar.dma_start(nb_all[P - 1 : P, :], nb[0:1, :])
        q_raw = sbuf("q_raw", [P, PACK, NQ], F32)
        nc.sync.dma_start(q_raw[:], qT[0].rearrange("(p j) q -> p j q", j=PACK))
        nc.sync.dma_start(us_row[:], us[0].rearrange("i o -> o i"))
        k_all = sbuf("k_all", [P, T], I32)
        nc.sync.dma_start(k_all[:], words_view(k_words))
        c_all = sbuf("c_all", [P, T], I32)
        nc.sync.dma_start(c_all[:, 0:AHEAD], words_view(c_words)[:, 0:AHEAD])
        nc.scalar.activation(warm[:, 1:2], warm[:, 0:1], ACT.Silu)

        listed_planes = sbuf("listed_planes", [P, 2, PACK, P], U8)
        for side, table in enumerate((k_table, c_table)):
            nc.vector.tensor_copy(listed_planes[:, side].rearrange("p t m -> p m t"), table[:].indirect(offsets[:]))
        planes = sbuf("planes", [P, 2, PACK, P], U8, "k_table")
        plane_words = planes[:].rearrange("p s t m -> p (s t m)").bitcast(I32)
        nc.gpsimd.memset(plane_words, 0)
        ident = sbuf("ident", [P, P], F32, "k_table", 1024)
        make_identity(nc, ident[:])
        listed_words = listed_planes[:].rearrange("p s t m -> p (s t m)").bitcast(I32)
        for r in range(4):
            nc.sync.dma_start(plane_words[r:P:32, :], listed_words[P - ROWS + r : P : 4, :])
        nc.sync.dma_start(c_all[:, AHEAD:T], words_view(c_words)[:, AHEAD:T])
        v_all = []
        for j in range(DV // P):
            v_all.append(sbuf("v_all%d" % j, [P, T], F32))
            nc.sync.dma_start(v_all[j][:], vT[blocks[j], :])

        rows = sbuf("rows", [P, N], F32)
        nc.scalar.activation(rows[:], nb_all[:].indirect(offsets[:]), ACT.Copy)
        q_bf = [sbuf("q_bf%d" % g, [P, HALF, PACK], BF16) for g in range(2)]
        for g in range(2):
            nc.scalar.copy(
                q_bf[g][:].rearrange("p (c i) t -> p c t i", i=RUN),
                q_raw[:, :, halves[g]].rearrange("p t (c i) -> p c t i", i=RUN),
            )
        nc.vector.tensor_copy(rows[0:1, :], us_row[:])
        rows_ps = bank(4, [P, PACK, P], "rows_ps")
        for t in range(PACK):
            nc.tensor.transpose(rows_ps[:, t, :], rows[:, t:N:PACK], ident[:])
        cols = sbuf("cols", [P, PACK, 2], F32, "q_raw")
        nc.scalar.copy(cols[:], rows_ps[:, :, 0 : P : P - 1])

        def gather_words(window, name):
            words = sbuf(name, [P, PACK, P], U32)
            nc.vector.tensor_copy(words[:].rearrange("p t m -> p m t"), window[:].bitcast(U32).indirect(offsets[:]))
            return words

        q_plane = sbuf("q_plane", [P, NQ], U8)
        q_codes = [sbuf("q_codes0", [P, HALF], U32, "nb_all")]
        quantize(q_codes[0][:], q_plane[:, halves[0]], q_bf[0][:])
        k_codes = gather_words(k_all, "k_codes")
        q_codes.append(sbuf("q_codes1", [P, HALF], U32, "k_all"))
        quantize(q_codes[1][:], q_plane[:, halves[1]], q_bf[1][:])
        c_codes = gather_words(c_all, "c_codes")

        gated = [sbuf("gated%d" % g, [P, PACK, HALF], F32) for g in range(2)]
        scaled = [sbuf("scaled%d" % g, [P, PACK, HALF], F32) for g in range(2)]
        for g in range(2):
            for t in range(PACK):
                a_ps = bank(PACK * g + t, [P, HALF], "a_ps")
                matmul(a_ps[:], k_codes[:, t, :], planes[:, 0, t, :], q_codes[g][:], q_plane[:, halves[g]])
                nc.scalar.activation(gated[g][:, t, :], a_ps[:], ACT.Silu, bias=cols[:, t, 1:2])
        for g in range(2):
            for t in range(2):
                nc.gpsimd.tensor_scalar(
                    out=scaled[g][:, t, :], in0=gated[g][:, t, :], scalar1=cols[:, t, 0:1], scalar2=0.0, op0=ALU.mult, op1=ALU.add
                )
        for t in range(2, PACK):
            nc.vector.tensor_scalar(out=scaled[0][:, t, :], in0=gated[0][:, t, :], scalar1=cols[:, t, 0:1], scalar2=None, op0=ALU.mult)
            nc.scalar.activation(scaled[1][:, t, :], gated[1][:, t, :], ACT.Copy, scale=cols[:, t, 0:1])

        y_bf = [sbuf("y_bf%d" % g, [P, HALF, PACK], BF16) for g in range(2)]
        for b in range(NQ // P):
            g, within = divmod(b, 2)
            z_ps = bank(b, [P, PACK, P], "z_ps")
            for t in range(PACK):
                matmul(z_ps[:, t, :], c_codes[:, t, :], planes[:, 1, t, :], q_codes[g][:, blocks[within]], q_plane[:, blocks[b]])
            nc.vector.tensor_tensor(
                y_bf[g][:, blocks[within], :].rearrange("p (c i) t -> p c t i", i=2),
                z_ps[:].rearrange("p t (c i) -> p c t i", i=2),
                scaled[g][:, :, blocks[within]].rearrange("p t (c i) -> p c t i", i=2),
                ALU.mult,
            )
        y_codes = sbuf("y_codes", [P, NQ], U32)
        y_plane = sbuf("y_plane", [P, NQ], U8)
        v_plane = sbuf("v_plane", [P, DV], U8)

        def gather_values(j, over=None):
            listed = sbuf("v_listed%d" % j, [P, N], BF16, over)
            share = SHARE[j]
            if share > 0:
                nc.vector.tensor_copy(listed[:, 0 : 16 * share], v_all[j][:].indirect(offsets[:, 0:share]))
            nc.scalar.activation(listed[:, 16 * share : N], v_all[j][:].indirect(offsets[:, share:COLS]), ACT.Copy)
            return listed

        def turn_values(j, listed, over=None):
            words = listed[:].bitcast(F32)
            turned = bank(PACK + j, [P, 2, P], "v_turned")
            for u in range(2):
                nc.tensor.transpose(turned[:, u, :], words[:, u : N // 2 : 2], ident[:])
            staged = sbuf("v_bf%d" % j, [P, P, PACK], BF16, over)
            dst = staged[:].rearrange("p e t -> p (e t)").bitcast(F32)
            nc.scalar.copy(dst.rearrange("p (e u) -> p e u", u=2), turned[:].rearrange("p u e -> p e u"))
            return staged

        def multiply(j, staged, sums, over=None, at=0):
            codes = sbuf("v_codes%d" % j, [P, P], U32, over, at)
            quantize(codes[:], v_plane[:, blocks[j]], staged[:])
            for b in range(NQ // P):
                matmul(sums[b], y_codes[:, blocks[b]], y_plane[:, blocks[b]], codes[:], v_plane[:, blocks[j]])

        out_view = out[0].rearrange("(b p) e -> p b e", p=P)

        def store(name, rows_at, cols_at, sums, copy, queue, over=None, at=0):
            res = sbuf(name, list(sums.shape), F32, over, at)
            copy(res[:], sums[:, :, :])
            queue.dma_start(out_view[:, rows_at, cols_at], res[:])

        listed0 = gather_values(0, "k_codes")
        for g in range(2):
            quantize(y_codes[:, halves[g]], y_plane[:, halves[g]], y_bf[g][:])
        listed1 = gather_values(1)
        v_bf0 = turn_values(0, listed0, "v_all1")
        copies = (nc.vector.tensor_copy, nc.scalar.copy)
        first = [bank(g, [P, 2, P], "first") for g in range(2)]
        multiply(0, v_bf0, [first[b // 2][:, b % 2, :] for b in range(4)])
        listed2 = gather_values(2)
        v_bf1 = turn_values(1, listed1, "v_all2")
        res_first = sbuf("res_first", [P, 4, P], F32, "v_all2", 2048)
        copies[1](res_first[:, 0:2, :], first[0][:])
        v_bf2 = turn_values(2, listed2)
        second = [bank(2 + g, [P, 2, P], "second") for g in range(2)]
        multiply(1, v_bf1, [second[b // 2][:, b % 2, :] for b in range(4)])
        copies[0](res_first[:, 2:4, :], first[1][:])
        nc.sync.dma_start(out_view[:, :, blocks[0]], res_first[:])
        listed3 = gather_values(3)
        v_bf3 = turn_values(3, listed3)
        third = [bank(g, [P, 2, P], "third") for g in range(2)]
        multiply(2, v_bf2, [third[b // 2][:, b % 2, :] for b in range(4)], "v_all3", 4096)
        for g in range(2):
            store("res_second%d" % g, slice(2 * g, 2 * g + 2), blocks[1], second[g], copies[1 - g], nc.sync, "v_all3", 1024 * g)
        last = [bank(index, [P, P], "last") for index in (4, 5, 6, 2)]
        multiply(3, v_bf3, [tile[:] for tile in last])
        store("res_third0", slice(0, 2), blocks[2], third[0], copies[1], nc.sync)
        store("res_third1", slice(2, 4), blocks[2], third[1], copies[0], nc.sync, "v_bf3")
        for g in range(2):
            res = sbuf("res_last%d" % g, [P, 2, P], F32)
            for w in range(2):
                copies[w](res[:, w, :], last[2 * g + w][:])
            nc.sync.dma_start(out_view[:, 2 * g : 2 * g + 2, blocks[3]], res[:])
